import numpy as np
import ml_dtypes


def mxq(x, axis, fmt="e4m3"):
    dtype, down = {"e4m3": (ml_dtypes.float8_e4m3fn, 7), "e5m2": (ml_dtypes.float8_e5m2, 14)}[fmt]
    v = np.moveaxis(np.asarray(x, np.float32).astype(ml_dtypes.bfloat16).astype(np.float64), axis, -1)
    blocks = v.reshape(v.shape[:-1] + (-1, 32))
    amax = np.abs(blocks).max(-1, keepdims=True)
    byte = np.maximum(np.where(amax > 0, np.frexp(amax)[1] - 1 + 127, 0) - down, 1)
    scale = np.exp2(byte - 127.0)
    codes = (blocks / scale).astype(np.float32).astype(dtype).astype(np.float64)
    return np.moveaxis((codes * scale).reshape(v.shape), -1, axis)


WIDE = False


def mx_kscale(k):
    if not WIDE:
        return np.ones(k)
    levels = np.array([10, -10, 5, -5, 0])
    if k % 512:
        return np.exp2(np.random.permutation(np.resize(levels, k // 32))).repeat(32)
    a = np.empty((k // 512, 16))
    for p in range(k // 512):
        a[p, :8] = np.random.permutation(np.resize(levels, 8))
        for g in range(8):
            far = levels[np.abs(levels - a[p, g]) >= 10]
            a[p, g + 8] = far[np.random.randint(len(far))]
    return np.exp2(a.ravel()).repeat(32)


def f64(x):
    return np.asarray(x).astype(np.float64)


def striped(idx):
    return np.tile(idx.reshape(-1, 16).T, (8, 1)).astype(np.uint16)


def unstriped(offs):
    return offs[:16].T.reshape(-1).astype(np.int64)


def pack_weight(w):
    k, n = w.shape
    w = f64(np.asarray(w, np.float32).astype(ml_dtypes.bfloat16)).reshape(k // 32, 32, n)
    amax = np.abs(w).max(1)
    byte = np.clip(np.where(amax > 0, np.frexp(amax)[1] - 1 + 127 - 7, 1), 1, 254)
    scaled = (w * np.exp2(127.0 - byte)[:, None, :]).reshape(k, n).astype(np.float32)
    words = np.ascontiguousarray(scaled.reshape(k // 512, 128, 4, n).transpose(0, 1, 3, 2)).astype(ml_dtypes.float8_e4m3fn).view(np.uint8)
    return words, np.ascontiguousarray(byte.astype(np.uint8).reshape(k // 512, 16, n))


def unpack_weight(words, scales):
    g, p, n, _ = words.shape
    vals = np.ascontiguousarray(words).view(ml_dtypes.float8_e4m3fn).astype(np.float64) * np.repeat(np.exp2(scales.astype(np.float64) - 127.0), 8, axis=1)[..., None]
    return vals.transpose(0, 1, 3, 2).reshape(g * 512, n)


K, T, S, H, N = 1024, 2048, 1024, 512, 128


def setup_inputs():
    n = np.random.standard_normal
    s = mx_kscale(K)[:, None]
    u = mx_kscale(H)
    packed_w2 = pack_weight(n((H, N)) / np.sqrt(H) / u[:, None])
    return {
        "xT": (n((K, T)) * s).astype(np.float32),
        "w1": (n((K, H)) / np.sqrt(K) / s * u).astype(np.float32),
        "w2_words": packed_w2[0],
        "w2_scales": packed_w2[1],
        "pos": (0.5 * n((H, S)) * u[:, None]).astype(np.float32),
        "offs": striped(np.random.permutation(T)[(T * np.random.uniform(0, 1, S) ** 4).astype(np.int64)]),
    }


def reference(xT, w1, w2_words, w2_scales, pos, offs):
    xq = mxq(f64(xT)[:, unstriped(offs)], 0, "e4m3")
    h = (mxq(f64(w1), 0, "e4m3").T @ xq) + f64(pos)
    return unpack_weight(w2_words, w2_scales).T @ mxq(h, 0, "e4m3")

@@ -1,0 +1,176 @@
+from contextlib import ExitStack
+
+import concourse.mybir as mybir
+
+K, T, S, H, N = 1024, 2048, 1024, 512, 128
+FLOPS = 2 * K * H * S + 2 * H * N * S
+
+F32 = mybir.dt.float32
+BF16 = mybir.dt.bfloat16
+I32 = mybir.dt.int32
+U32 = mybir.dt.uint32
+U16 = mybir.dt.uint16
+U8 = mybir.dt.uint8
+FP8X4 = mybir.dt.float8_e4m3fn_x4
+COPY = mybir.ActivationFunctionType.Copy
+ADD = mybir.AluOpType.add
+
+P = 128
+PACK = 4
+K_PASS = P * PACK
+PASSES = K // K_PASS
+RUN = 2
+GROUP = 128
+HALF = S // 2
+
+X_LOADS = (
+    (((512, 0), (0, 512)), ((256, 256),), ((192, 320),)),
+    (((512, 0),), ((256, 256),), ((192, 320),), ((128, 128),), ((128, 128),)),
+)
+OUT_PIECES = (256, 256, 256, 128, 128)
+
+
+def tile_picked_embpos_none_e_kernel(tc, xT, w1, w2_words, w2_scales, pos, offs, out):
+    nc = tc.nc
+    with ExitStack() as ctx:
+        keep = ctx.enter_context(tc.tile_pool(name="keep", bufs=1))
+        h_psum = ctx.enter_context(tc.psum_pool(name="h_psum", bufs=6))
+        o_psum = ctx.enter_context(tc.psum_pool(name="o_psum", bufs=2))
+
+        offsets = keep.tile([P, S // 16], U16, name="offsets")
+        x_words = [keep.tile([P, T], U32, name="x_words%d" % g, align_bytes=64) for g in range(PASSES)]
+        x_scales = keep.tile([P, T], U8, name="x_scales", align_bytes=64)
+        w2_codes = keep.tile([P, N], U32, name="w2_codes", align_bytes=64)
+        w2_bytes = keep.tile([P, N], U8, name="w2_bytes", align_bytes=64)
+
+        nc.gpsimd.memset(x_scales[:], 0)
+        nc.gpsimd.memset(w2_bytes[:], 0)
+        nc.gpsimd.dma_start(out=w2_codes[:].bitcast(I32), in_=w2_words[0].rearrange("p n t -> p (n t)").bitcast(I32))
+        for q in range(4):
+            nc.gpsimd.dma_start(
+                out=w2_bytes[32 * q : 32 * q + 4, :].bitcast(I32),
+                in_=w2_scales[0][4 * q : 4 * q + 4, :].bitcast(I32),
+            )
+
+        x_raw = []
+        for g in range(PASSES):
+            rows = xT[g * K_PASS : (g + 1) * K_PASS, :].rearrange("(p j) s -> p j s", j=PACK)
+            first = 0
+            for shares in X_LOADS[g]:
+                width = sum(a + b for a, b in shares)
+                raw = keep.tile([P, PACK, width], F32, name="x_raw%d_%d" % (g, first))
+                nc.sync.dma_start(out=raw[:], in_=rows[:, :, first : first + width])
+                if g == 0 and first == 0:
+                    nc.sync.dma_start(offsets[:], offs)
+                x_raw.append((g, first, raw, shares))
+                first = first + width
+
+        w1_raw = []
+        for g in range(PASSES):
+            rows = w1[g * K_PASS : (g + 1) * K_PASS, :].rearrange("(p j) i -> p j i", j=PACK)
+            for u in range(2):
+                raw = keep.tile([P, PACK, H // 2], F32, name="w1_raw%d_%d" % (g, u))
+                nc.sync.dma_start(out=raw[:], in_=rows[:, :, u * (H // 2) : (u + 1) * (H // 2)])
+                w1_raw.append(raw)
+
+        pos_rows = pos.rearrange("(p t) s -> p t s", t=PACK)
+        pos_sb = []
+        for u in range(2):
+            half = keep.tile([P, PACK, HALF], F32, name="pos%d" % u)
+            nc.sync.dma_start(out=half[:], in_=pos_rows[:, :, u * HALF : (u + 1) * HALF])
+            pos_sb.append(half)
+
+        picked_scales = {}
+
+        def gather(table, dtype, picked, first, n, tag):
+            tile = keep.tile([P, n], dtype, name="picked", tag=tag, align_bytes=64)
+            nc.vector.tensor_copy(tile[:], table[:].indirect(offsets[:, first // 16 : (first + n) // 16]))
+            for at in range(0, n, GROUP):
+                picked[first + at] = (tile, slice(at, at + GROUP))
+
+        picked_words = [{}, {}]
+        for g, first, raw, shares in x_raw:
+            at = 0
+            for on_scalar, on_vector in shares:
+                n = on_scalar + on_vector
+                rounded = keep.tile([P, n * PACK], BF16, name="x_bf%d_%d" % (g, first + at), align_bytes=64)
+                dst = rounded[:].rearrange("p (c i j) -> p c j i", i=RUN, j=PACK)
+                src = raw[:, :, at : at + n].rearrange("p j (c i) -> p c j i", i=RUN)
+                cut = on_scalar // RUN
+                if on_scalar:
+                    nc.scalar.activation(out=dst[:, :cut], in_=src[:, :cut], func=COPY)
+                if on_vector:
+                    nc.vector.tensor_copy(out=dst[:, cut:], in_=src[:, cut:])
+                cols = slice(first + at, first + at + n)
+                nc.vector.quantize_mx(out=x_words[g][:, cols].bitcast(FP8X4), scales=x_scales[4 * g : P, cols], in_=rounded[:])
+                at = at + n
+            if g == 0 and first + at == T:
+                gather(x_words[0], U32, picked_words[0], 0, S, "picked_words0")
+
+        def quantise_w1(g):
+            rounded = keep.tile([P, H * PACK], BF16, name="w1_bf", tag="w1_bf%d" % g, align_bytes=64)
+            dealt = rounded[:].rearrange("p (a b m j) -> p a m j b", a=2, b=2, j=PACK)
+            for u in range(2):
+                src = w1_raw[2 * g + u][:].rearrange("p j (m a b) -> p a m j b", a=2, b=2)
+                nc.scalar.copy(out=dealt[:, :, u * 64 : (u + 1) * 64, :, :], in_=src)
+            codes = keep.tile([P, H], U32, name="w1_codes%d" % g, align_bytes=64)
+            scale_bytes = keep.tile([P, H], U8, name="w1_bytes%d" % g, align_bytes=64)
+            nc.vector.quantize_mx(out=codes[:].bitcast(FP8X4), scales=scale_bytes[:], in_=rounded[:])
+            return codes, scale_bytes
+
+        gather(x_words[1], U32, picked_words[1], 0, HALF, "picked_words1")
+        gather(x_scales, U8, picked_scales, 0, HALF + HALF // 2, "picked_scales")
+        w1_first = quantise_w1(0)
+        warm = o_psum.tile([P, H], F32, name="res")
+        for k in range(3):
+            nc.tensor.matmul_mx(out=warm[:], lhsT=w1_first[0][:, :P].bitcast(FP8X4), lhsT_scale=w1_first[1][:, :P], rhs=w1_first[0][:].bitcast(FP8X4), rhs_scale=w1_first[1][:], start=True, stop=True)
+        gather(x_words[1], U32, picked_words[1], HALF, HALF, "w1_bf0")
+        w1_second = quantise_w1(1)
+        gather(x_scales, U8, picked_scales, HALF + HALF // 2, HALF // 2, "w1_bf1")
+        w1_codes = (w1_first[0], w1_second[0])
+        w1_bytes = (w1_first[1], w1_second[1])
+
+        first = 0
+        for n in OUT_PIECES:
+            h_bf = keep.tile([P, n * PACK], BF16, name="h_bf%d" % first, align_bytes=64)
+            for at in range(0, n, GROUP):
+                u, within = divmod(first + at, HALF)
+                cols = slice(within, within + GROUP)
+                acc = h_psum.tile([P, PACK, GROUP], F32, name="acc")
+                for t in range(PACK):
+                    chans = slice(t * P, (t + 1) * P)
+                    for g in range(PASSES):
+                        words, word_cols = picked_words[g][first + at]
+                        scale_rows, scale_cols = picked_scales[first + at]
+                        nc.tensor.matmul_mx(
+                            out=acc[:, t, :],
+                            lhsT=w1_codes[g][:, chans].bitcast(FP8X4),
+                            lhsT_scale=w1_bytes[g][:, chans],
+                            rhs=words[:, word_cols].bitcast(FP8X4),
+                            rhs_scale=scale_rows[4 * g : P, scale_cols],
+                            start=(g == 0),
+                            stop=(g == PASSES - 1),
+                        )
+                nc.vector.tensor_tensor(
+                    out=h_bf[:, at * PACK : (at + GROUP) * PACK].rearrange("p (c i t) -> p c t i", i=RUN, t=PACK),
+                    in0=acc[:].rearrange("p t (c i) -> p c t i", i=RUN),
+                    in1=pos_sb[u][:, :, cols].rearrange("p t (c i) -> p c t i", i=RUN),
+                    op=ADD,
+                )
+            h_codes = keep.tile([P, n], U32, name="h_codes%d" % first, align_bytes=64)
+            h_bytes = keep.tile([P, n], U8, name="h_bytes%d" % first, align_bytes=64)
+            nc.vector.quantize_mx(out=h_codes[:].bitcast(FP8X4), scales=h_bytes[:], in_=h_bf[:])
+            res = o_psum.tile([P, n], F32, name="res")
+            nc.tensor.matmul_mx(
+                out=res[:],
+                lhsT=w2_codes[:].bitcast(FP8X4),
+                lhsT_scale=w2_bytes[:],
+                rhs=h_codes[:].bitcast(FP8X4),
+                rhs_scale=h_bytes[:],
+                start=True,
+                stop=True,
+            )
+            staged = keep.tile([P, n], F32, name="staged%d" % first)
+            nc.scalar.copy(out=staged[:], in_=res[:])
+            nc.sync.dma_start(out=out[:, first : first + n], in_=staged[:])
+            first = first + n

@@ -24,8 +24,8 @@ GROUP = 128
 HALF = S // 2
 
 X_LOADS = (
-    (((512, 0), (0, 512)), ((256, 256),), ((192, 320),)),
-    (((512, 0),), ((256, 256),), ((192, 320),), ((128, 128),), ((128, 128),)),
+    (((512, 0), (0, 512)), ((0, 512), (512, 0))),
+    (((0, 512), (512, 0)), ((256, 256),), ((256, 0),), ((128, 128),)),
 )
 OUT_PIECES = (256, 256, 256, 128, 128)
 
@@ -45,12 +45,6 @@ def tile_picked_embpos_none_e_kernel(tc, xT, w1, w2_words, w2_scales, pos, offs,
 
         nc.gpsimd.memset(x_scales[:], 0)
         nc.gpsimd.memset(w2_bytes[:], 0)
-        nc.gpsimd.dma_start(out=w2_codes[:].bitcast(I32), in_=w2_words[0].rearrange("p n t -> p (n t)").bitcast(I32))
-        for q in range(4):
-            nc.gpsimd.dma_start(
-                out=w2_bytes[32 * q : 32 * q + 4, :].bitcast(I32),
-                in_=w2_scales[0][4 * q : 4 * q + 4, :].bitcast(I32),
-            )
 
         x_raw = []
         for g in range(PASSES):
@@ -68,10 +62,9 @@ def tile_picked_embpos_none_e_kernel(tc, xT, w1, w2_words, w2_scales, pos, offs,
         w1_raw = []
         for g in range(PASSES):
             rows = w1[g * K_PASS : (g + 1) * K_PASS, :].rearrange("(p j) i -> p j i", j=PACK)
-            for u in range(2):
-                raw = keep.tile([P, PACK, H // 2], F32, name="w1_raw%d_%d" % (g, u))
-                nc.sync.dma_start(out=raw[:], in_=rows[:, :, u * (H // 2) : (u + 1) * (H // 2)])
-                w1_raw.append(raw)
+            raw = keep.tile([P, PACK, H], F32, name="w1_raw%d" % g)
+            nc.sync.dma_start(out=raw[:], in_=rows)
+            w1_raw.append(raw)
 
         pos_rows = pos.rearrange("(p t) s -> p t s", t=PACK)
         pos_sb = []
@@ -79,6 +72,14 @@ def tile_picked_embpos_none_e_kernel(tc, xT, w1, w2_words, w2_scales, pos, offs,
             half = keep.tile([P, PACK, HALF], F32, name="pos%d" % u)
             nc.sync.dma_start(out=half[:], in_=pos_rows[:, :, u * HALF : (u + 1) * HALF])
             pos_sb.append(half)
+            if u == 0:
+                nc.sync.dma_start(out=w2_codes[:].bitcast(I32), in_=w2_words[0].rearrange("p n t -> p (n t)").bitcast(I32))
+                for q in range(4):
+                    nc.sync.dma_start(
+                        out=w2_bytes[32 * q : 32 * q + 4, :].bitcast(I32),
+                        in_=w2_scales[0][4 * q : 4 * q + 4, :].bitcast(I32),
+                    )
+
 
         picked_scales = {}
 
@@ -107,12 +108,13 @@ def tile_picked_embpos_none_e_kernel(tc, xT, w1, w2_words, w2_scales, pos, offs,
             if g == 0 and first + at == T:
                 gather(x_words[0], U32, picked_words[0], 0, S, "picked_words0")
 
-        def quantise_w1(g):
+        def quantise_w1(g, on_scalar):
             rounded = keep.tile([P, H * PACK], BF16, name="w1_bf", tag="w1_bf%d" % g, align_bytes=64)
             dealt = rounded[:].rearrange("p (a b m j) -> p a m j b", a=2, b=2, j=PACK)
-            for u in range(2):
-                src = w1_raw[2 * g + u][:].rearrange("p j (m a b) -> p a m j b", a=2, b=2)
-                nc.scalar.copy(out=dealt[:, :, u * 64 : (u + 1) * 64, :, :], in_=src)
+            src = w1_raw[g][:].rearrange("p j (m a b) -> p a m j b", a=2, b=2)
+            nc.scalar.copy(out=dealt[:, :, :on_scalar], in_=src[:, :, :on_scalar])
+            if on_scalar < P:
+                nc.vector.tensor_copy(out=dealt[:, :, on_scalar:], in_=src[:, :, on_scalar:])
             codes = keep.tile([P, H], U32, name="w1_codes%d" % g, align_bytes=64)
             scale_bytes = keep.tile([P, H], U8, name="w1_bytes%d" % g, align_bytes=64)
             nc.vector.quantize_mx(out=codes[:].bitcast(FP8X4), scales=scale_bytes[:], in_=rounded[:])
@@ -120,12 +122,12 @@ def tile_picked_embpos_none_e_kernel(tc, xT, w1, w2_words, w2_scales, pos, offs,
 
         gather(x_words[1], U32, picked_words[1], 0, HALF, "picked_words1")
         gather(x_scales, U8, picked_scales, 0, HALF + HALF // 2, "picked_scales")
-        w1_first = quantise_w1(0)
+        w1_first = quantise_w1(0, P)
         warm = o_psum.tile([P, H], F32, name="res")
         for k in range(3):
             nc.tensor.matmul_mx(out=warm[:], lhsT=w1_first[0][:, :P].bitcast(FP8X4), lhsT_scale=w1_first[1][:, :P], rhs=w1_first[0][:].bitcast(FP8X4), rhs_scale=w1_first[1][:], start=True, stop=True)
         gather(x_words[1], U32, picked_words[1], HALF, HALF, "w1_bf0")
-        w1_second = quantise_w1(1)
+        w1_second = quantise_w1(1, 96)
         gather(x_scales, U8, picked_scales, HALF + HALF // 2, HALF // 2, "w1_bf1")
         w1_codes = (w1_first[0], w1_second[0])
         w1_bytes = (w1_first[1], w1_second[1])

@@ -25,17 +25,16 @@ HALF = S // 2
 
 X_LOADS = (
     (((512, 0), (0, 512)), ((0, 512), (512, 0))),
-    (((0, 512), (512, 0)), ((256, 256),), ((256, 0),), ((128, 128),)),
+    (((512, 0),), ((384, 128),), ((320, 192),), ((192, 64),), ((128, 128),)),
 )
-OUT_PIECES = (256, 256, 256, 128, 128)
+OUT_PIECES = ((512,), (256, 128, 128))
 
 
 def tile_picked_embpos_none_e_kernel(tc, xT, w1, w2_words, w2_scales, pos, offs, out):
     nc = tc.nc
     with ExitStack() as ctx:
         keep = ctx.enter_context(tc.tile_pool(name="keep", bufs=1))
-        h_psum = ctx.enter_context(tc.psum_pool(name="h_psum", bufs=6))
-        o_psum = ctx.enter_context(tc.psum_pool(name="o_psum", bufs=2))
+        psum = ctx.enter_context(tc.psum_pool(name="psum", bufs=8))
 
         offsets = keep.tile([P, S // 16], U16, name="offsets")
         x_words = [keep.tile([P, T], U32, name="x_words%d" % g, align_bytes=64) for g in range(PASSES)]
@@ -72,13 +71,12 @@ def tile_picked_embpos_none_e_kernel(tc, xT, w1, w2_words, w2_scales, pos, offs,
             half = keep.tile([P, PACK, HALF], F32, name="pos%d" % u)
             nc.sync.dma_start(out=half[:], in_=pos_rows[:, :, u * HALF : (u + 1) * HALF])
             pos_sb.append(half)
-            if u == 0:
-                nc.sync.dma_start(out=w2_codes[:].bitcast(I32), in_=w2_words[0].rearrange("p n t -> p (n t)").bitcast(I32))
-                for q in range(4):
-                    nc.sync.dma_start(
-                        out=w2_bytes[32 * q : 32 * q + 4, :].bitcast(I32),
-                        in_=w2_scales[0][4 * q : 4 * q + 4, :].bitcast(I32),
-                    )
+        nc.sync.dma_start(out=w2_codes[:].bitcast(I32), in_=w2_words[0].rearrange("p n t -> p (n t)").bitcast(I32))
+        for q in range(4):
+            nc.sync.dma_start(
+                out=w2_bytes[32 * q : 32 * q + 4, :].bitcast(I32),
+                in_=w2_scales[0][4 * q : 4 * q + 4, :].bitcast(I32),
+            )
 
 
         picked_scales = {}
@@ -108,61 +106,74 @@ def tile_picked_embpos_none_e_kernel(tc, xT, w1, w2_words, w2_scales, pos, offs,
             if g == 0 and first + at == T:
                 gather(x_words[0], U32, picked_words[0], 0, S, "picked_words0")
 
-        def quantise_w1(g, on_scalar):
-            rounded = keep.tile([P, H * PACK], BF16, name="w1_bf", tag="w1_bf%d" % g, align_bytes=64)
-            dealt = rounded[:].rearrange("p (a b m j) -> p a m j b", a=2, b=2, j=PACK)
+        w1_codes = {}
+
+        def quantise_w1(g, a, pairs, tag):
+            rounded = keep.tile([P, pairs * 2 * P * PACK], BF16, name="w1_bf", tag=tag, align_bytes=64)
+            dealt = rounded[:].rearrange("p (a b m j) -> p a m j b", a=pairs, b=2, j=PACK)
             src = w1_raw[g][:].rearrange("p j (m a b) -> p a m j b", a=2, b=2)
-            nc.scalar.copy(out=dealt[:, :, :on_scalar], in_=src[:, :, :on_scalar])
-            if on_scalar < P:
-                nc.vector.tensor_copy(out=dealt[:, :, on_scalar:], in_=src[:, :, on_scalar:])
-            codes = keep.tile([P, H], U32, name="w1_codes%d" % g, align_bytes=64)
-            scale_bytes = keep.tile([P, H], U8, name="w1_bytes%d" % g, align_bytes=64)
+            nc.scalar.copy(out=dealt, in_=src[:, a : a + pairs])
+            codes = keep.tile([P, pairs * 2 * P], U32, name="w1_codes%d_%d" % (g, a), align_bytes=64)
+            scale_bytes = keep.tile([P, pairs * 2 * P], U8, name="w1_bytes%d_%d" % (g, a), align_bytes=64)
             nc.vector.quantize_mx(out=codes[:].bitcast(FP8X4), scales=scale_bytes[:], in_=rounded[:])
-            return codes, scale_bytes
+            for t in range(2 * pairs):
+                w1_codes[g, 2 * a + t] = (codes[:, t * P : (t + 1) * P], scale_bytes[:, t * P : (t + 1) * P])
 
+        gather(x_scales, U8, picked_scales, 0, HALF, "picked_scales0")
+        gather(x_scales, U8, picked_scales, HALF, HALF, "picked_scales1")
         gather(x_words[1], U32, picked_words[1], 0, HALF, "picked_words1")
-        gather(x_scales, U8, picked_scales, 0, HALF + HALF // 2, "picked_scales")
-        w1_first = quantise_w1(0, P)
-        warm = o_psum.tile([P, H], F32, name="res")
-        for k in range(3):
-            nc.tensor.matmul_mx(out=warm[:], lhsT=w1_first[0][:, :P].bitcast(FP8X4), lhsT_scale=w1_first[1][:, :P], rhs=w1_first[0][:].bitcast(FP8X4), rhs_scale=w1_first[1][:], start=True, stop=True)
-        gather(x_words[1], U32, picked_words[1], HALF, HALF, "w1_bf0")
-        w1_second = quantise_w1(1, 96)
-        gather(x_scales, U8, picked_scales, HALF + HALF // 2, HALF // 2, "w1_bf1")
-        w1_codes = (w1_first[0], w1_second[0])
-        w1_bytes = (w1_first[1], w1_second[1])
+        warm = psum.tile([P, HALF], F32, name="warm", tag="bank")
+        words = picked_words[0][0][0]
+        scale_rows = picked_scales[0][0]
+        for k in range(4):
+            nc.tensor.matmul_mx(out=warm[:], lhsT=words[:, :P].bitcast(FP8X4), lhsT_scale=scale_rows[:, :P], rhs=words[:, :HALF].bitcast(FP8X4), rhs_scale=scale_rows[:, :HALF], start=True, stop=True)
+        quantise_w1(0, 0, 2, "w1_bf0")
+        gather(x_words[1], U32, picked_words[1], HALF, HALF // 2, "w1_bf0")
+        quantise_w1(1, 0, 1, "w1_bf1")
+        quantise_w1(1, 1, 1, "w1_bf2")
+        gather(x_words[1], U32, picked_words[1], HALF + HALF // 2, HALF // 2, "w1_bf2")
 
-        first = 0
-        for n in OUT_PIECES:
-            h_bf = keep.tile([P, n * PACK], BF16, name="h_bf%d" % first, align_bytes=64)
-            for at in range(0, n, GROUP):
-                u, within = divmod(first + at, HALF)
-                cols = slice(within, within + GROUP)
-                acc = h_psum.tile([P, PACK, GROUP], F32, name="acc")
-                for t in range(PACK):
-                    chans = slice(t * P, (t + 1) * P)
-                    for g in range(PASSES):
-                        words, word_cols = picked_words[g][first + at]
-                        scale_rows, scale_cols = picked_scales[first + at]
-                        nc.tensor.matmul_mx(
-                            out=acc[:, t, :],
-                            lhsT=w1_codes[g][:, chans].bitcast(FP8X4),
-                            lhsT_scale=w1_bytes[g][:, chans],
-                            rhs=words[:, word_cols].bitcast(FP8X4),
-                            rhs_scale=scale_rows[4 * g : P, scale_cols],
-                            start=(g == 0),
-                            stop=(g == PASSES - 1),
-                        )
-                nc.vector.tensor_tensor(
-                    out=h_bf[:, at * PACK : (at + GROUP) * PACK].rearrange("p (c i t) -> p c t i", i=RUN, t=PACK),
-                    in0=acc[:].rearrange("p t (c i) -> p c t i", i=RUN),
-                    in1=pos_sb[u][:, :, cols].rearrange("p t (c i) -> p c t i", i=RUN),
-                    op=ADD,
-                )
+        sums = {}
+        for first in range(0, S, GROUP):
+            acc = psum.tile([P, PACK, GROUP], F32, name="acc", tag="bank")
+            for t in (0, 1, 2, 3) if first < 3 * GROUP else (2, 3, 0, 1):
+                for g in range(PASSES):
+                    words, word_cols = picked_words[g][first]
+                    scale_rows, scale_cols = picked_scales[first]
+                    nc.tensor.matmul_mx(
+                        out=acc[:, t, :],
+                        lhsT=w1_codes[g, t][0].bitcast(FP8X4),
+                        lhsT_scale=w1_codes[g, t][1],
+                        rhs=words[:, word_cols].bitcast(FP8X4),
+                        rhs_scale=scale_rows[4 * g : P, scale_cols],
+                        start=(g == 0),
+                        stop=(g == PASSES - 1),
+                    )
+            sums[first] = acc
+
+        def add_pos(h_bf, at, first):
+            u, within = divmod(first, HALF)
+            rounded = h_bf[:, at * PACK : (at + GROUP) * PACK]
+            place = pos_sb[u][:, :, within : within + GROUP]
+            if within == 0:
+                place_rows = keep.tile([P, GROUP * PACK], F32, name="place_rows")
+                nc.scalar.copy(out=place_rows[:].rearrange("p (c i t) -> p c t i", i=RUN, t=PACK), in_=place.rearrange("p t (c i) -> p c t i", i=RUN))
+                product = keep.tile([P, GROUP * PACK], F32, name="product%d" % first)
+                nc.scalar.copy(out=product[:].rearrange("p (n t) -> p n t", t=PACK), in_=sums[first][:].rearrange("p t n -> p n t"))
+                nc.gpsimd.tensor_tensor(out=rounded, in0=product[:], in1=place_rows[:], op=ADD)
+                return
+            nc.vector.tensor_tensor(
+                out=rounded.rearrange("p (c i t) -> p c t i", i=RUN, t=PACK),
+                in0=sums[first][:].rearrange("p t (c i) -> p c t i", i=RUN),
+                in1=place.rearrange("p t (c i) -> p c t i", i=RUN),
+                op=ADD,
+            )
+
+        def second_layer(h_bf, first, n):
             h_codes = keep.tile([P, n], U32, name="h_codes%d" % first, align_bytes=64)
             h_bytes = keep.tile([P, n], U8, name="h_bytes%d" % first, align_bytes=64)
             nc.vector.quantize_mx(out=h_codes[:].bitcast(FP8X4), scales=h_bytes[:], in_=h_bf[:])
-            res = o_psum.tile([P, n], F32, name="res")
+            res = psum.tile([P, n], F32, name="res", tag="bank")
             nc.tensor.matmul_mx(
                 out=res[:],
                 lhsT=w2_codes[:].bitcast(FP8X4),
@@ -175,4 +186,15 @@ def tile_picked_embpos_none_e_kernel(tc, xT, w1, w2_words, w2_scales, pos, offs,
             staged = keep.tile([P, n], F32, name="staged%d" % first)
             nc.scalar.copy(out=staged[:], in_=res[:])
             nc.sync.dma_start(out=out[:, first : first + n], in_=staged[:])
-            first = first + n
+
+        first = 0
+        for pieces in OUT_PIECES:
+            ready = []
+            for n in pieces:
+                h_bf = keep.tile([P, n * PACK], BF16, name="h_bf%d" % first, align_bytes=64)
+                for at in range(0, n, GROUP):
+                    add_pos(h_bf, at, first + at)
+                ready.append((h_bf, first, n))
+                first = first + n
+            for piece in ready:
+                second_layer(*piece)

@@ -25,7 +25,7 @@ HALF = S // 2
 
 X_LOADS = (
     (((512, 0), (0, 512)), ((0, 512), (512, 0))),
-    (((512, 0),), ((384, 128),), ((320, 192),), ((192, 64),), ((128, 128),)),
+    (((256, 256), (512, 0)), ((128, 384),), ((128, 128),), ((128, 128),)),
 )
 OUT_PIECES = ((512,), (256, 128, 128))
 
@@ -122,11 +122,6 @@ def tile_picked_embpos_none_e_kernel(tc, xT, w1, w2_words, w2_scales, pos, offs,
         gather(x_scales, U8, picked_scales, 0, HALF, "picked_scales0")
         gather(x_scales, U8, picked_scales, HALF, HALF, "picked_scales1")
         gather(x_words[1], U32, picked_words[1], 0, HALF, "picked_words1")
-        warm = psum.tile([P, HALF], F32, name="warm", tag="bank")
-        words = picked_words[0][0][0]
-        scale_rows = picked_scales[0][0]
-        for k in range(4):
-            nc.tensor.matmul_mx(out=warm[:], lhsT=words[:, :P].bitcast(FP8X4), lhsT_scale=scale_rows[:, :P], rhs=words[:, :HALF].bitcast(FP8X4), rhs_scale=scale_rows[:, :HALF], start=True, stop=True)
         quantise_w1(0, 0, 2, "w1_bf0")
         gather(x_words[1], U32, picked_words[1], HALF, HALF // 2, "w1_bf0")
         quantise_w1(1, 0, 1, "w1_bf1")

@@ -19,15 +19,19 @@ P = 128
 PACK = 4
 K_PASS = P * PACK
 PASSES = K // K_PASS
+QUADRANT = 32
+PER_COLUMN = 16
 RUN = 2
 GROUP = 128
 HALF = S // 2
+QUARTER = S // 4
 
 X_LOADS = (
     (((512, 0), (0, 512)), ((0, 512), (512, 0))),
     (((256, 256), (512, 0)), ((128, 384),), ((128, 128),), ((128, 128),)),
 )
-OUT_PIECES = ((512,), (256, 128, 128))
+POS_LOADS = (HALF, QUARTER, QUARTER)
+EARLY_GROUPS = 3
 
 
 def tile_picked_embpos_none_e_kernel(tc, xT, w1, w2_words, w2_scales, pos, offs, out):
@@ -36,7 +40,7 @@ def tile_picked_embpos_none_e_kernel(tc, xT, w1, w2_words, w2_scales, pos, offs,
         keep = ctx.enter_context(tc.tile_pool(name="keep", bufs=1))
         psum = ctx.enter_context(tc.psum_pool(name="psum", bufs=8))
 
-        offsets = keep.tile([P, S // 16], U16, name="offsets")
+        offsets = keep.tile([P, S // PER_COLUMN], U16, name="offsets")
         x_words = [keep.tile([P, T], U32, name="x_words%d" % g, align_bytes=64) for g in range(PASSES)]
         x_scales = keep.tile([P, T], U8, name="x_scales", align_bytes=64)
         w2_codes = keep.tile([P, N], U32, name="w2_codes", align_bytes=64)
@@ -48,46 +52,48 @@ def tile_picked_embpos_none_e_kernel(tc, xT, w1, w2_words, w2_scales, pos, offs,
         x_raw = []
         for g in range(PASSES):
             rows = xT[g * K_PASS : (g + 1) * K_PASS, :].rearrange("(p j) s -> p j s", j=PACK)
-            first = 0
+            symbol = 0
             for shares in X_LOADS[g]:
-                width = sum(a + b for a, b in shares)
-                raw = keep.tile([P, PACK, width], F32, name="x_raw%d_%d" % (g, first))
-                nc.sync.dma_start(out=raw[:], in_=rows[:, :, first : first + width])
-                if g == 0 and first == 0:
+                width = sum(on_scalar + on_vector for on_scalar, on_vector in shares)
+                raw = keep.tile([P, PACK, width], F32, name="x_raw%d_%d" % (g, symbol))
+                nc.sync.dma_start(out=raw[:], in_=rows[:, :, symbol : symbol + width])
+                if not x_raw:
                     nc.sync.dma_start(offsets[:], offs)
-                x_raw.append((g, first, raw, shares))
-                first = first + width
+                x_raw.append((g, symbol, raw, shares))
+                symbol = symbol + width
 
         w1_raw = []
         for g in range(PASSES):
-            rows = w1[g * K_PASS : (g + 1) * K_PASS, :].rearrange("(p j) i -> p j i", j=PACK)
             raw = keep.tile([P, PACK, H], F32, name="w1_raw%d" % g)
-            nc.sync.dma_start(out=raw[:], in_=rows)
+            nc.sync.dma_start(out=raw[:], in_=w1[g * K_PASS : (g + 1) * K_PASS, :].rearrange("(p j) i -> p j i", j=PACK))
             w1_raw.append(raw)
 
         pos_rows = pos.rearrange("(p t) s -> p t s", t=PACK)
-        pos_sb = []
-        for u in range(2):
-            half = keep.tile([P, PACK, HALF], F32, name="pos%d" % u)
-            nc.sync.dma_start(out=half[:], in_=pos_rows[:, :, u * HALF : (u + 1) * HALF])
-            pos_sb.append(half)
-        nc.sync.dma_start(out=w2_codes[:].bitcast(I32), in_=w2_words[0].rearrange("p n t -> p (n t)").bitcast(I32))
-        for q in range(4):
-            nc.sync.dma_start(
-                out=w2_bytes[32 * q : 32 * q + 4, :].bitcast(I32),
-                in_=w2_scales[0][4 * q : 4 * q + 4, :].bitcast(I32),
-            )
+        pos_of = {}
+        entry = 0
+        for n in POS_LOADS:
+            raw = keep.tile([P, PACK, n], F32, name="pos%d" % entry)
+            nc.sync.dma_start(out=raw[:], in_=pos_rows[:, :, entry : entry + n])
+            for at in range(0, n, GROUP):
+                pos_of[entry + at] = raw[:, :, at : at + GROUP]
+            if entry == 0:
+                nc.sync.dma_start(out=w2_codes[:].bitcast(I32), in_=w2_words[0].rearrange("p n t -> p (n t)").bitcast(I32))
+                for q in range(P // QUADRANT):
+                    nc.sync.dma_start(
+                        out=w2_bytes[QUADRANT * q : QUADRANT * q + 4, :].bitcast(I32),
+                        in_=w2_scales[0][4 * q : 4 * q + 4, :].bitcast(I32),
+                    )
+            entry = entry + n
 
-
+        picked_words = [{} for g in range(PASSES)]
         picked_scales = {}
 
         def gather(table, dtype, picked, first, n, tag):
             tile = keep.tile([P, n], dtype, name="picked", tag=tag, align_bytes=64)
-            nc.vector.tensor_copy(tile[:], table[:].indirect(offsets[:, first // 16 : (first + n) // 16]))
+            nc.vector.tensor_copy(tile[:], table[:].indirect(offsets[:, first // PER_COLUMN : (first + n) // PER_COLUMN]))
             for at in range(0, n, GROUP):
                 picked[first + at] = (tile, slice(at, at + GROUP))
 
-        picked_words = [{}, {}]
         for g, first, raw, shares in x_raw:
             at = 0
             for on_scalar, on_vector in shares:
@@ -106,39 +112,40 @@ def tile_picked_embpos_none_e_kernel(tc, xT, w1, w2_words, w2_scales, pos, offs,
             if g == 0 and first + at == T:
                 gather(x_words[0], U32, picked_words[0], 0, S, "picked_words0")
 
-        w1_codes = {}
+        w1_tiles = {}
 
-        def quantise_w1(g, a, pairs, tag):
-            rounded = keep.tile([P, pairs * 2 * P * PACK], BF16, name="w1_bf", tag=tag, align_bytes=64)
-            dealt = rounded[:].rearrange("p (a b m j) -> p a m j b", a=pairs, b=2, j=PACK)
+        def quantise_w1(g, first_pair, pairs, tag):
+            columns = pairs * 2 * P
+            rounded = keep.tile([P, columns * PACK], BF16, name="w1_bf", tag=tag, align_bytes=64)
+            dst = rounded[:].rearrange("p (a b m j) -> p a m j b", a=pairs, b=2, j=PACK)
             src = w1_raw[g][:].rearrange("p j (m a b) -> p a m j b", a=2, b=2)
-            nc.scalar.copy(out=dealt, in_=src[:, a : a + pairs])
-            codes = keep.tile([P, pairs * 2 * P], U32, name="w1_codes%d_%d" % (g, a), align_bytes=64)
-            scale_bytes = keep.tile([P, pairs * 2 * P], U8, name="w1_bytes%d_%d" % (g, a), align_bytes=64)
+            nc.scalar.copy(out=dst, in_=src[:, first_pair : first_pair + pairs])
+            codes = keep.tile([P, columns], U32, name="w1_codes%d_%d" % (g, first_pair), align_bytes=64)
+            scale_bytes = keep.tile([P, columns], U8, name="w1_bytes%d_%d" % (g, first_pair), align_bytes=64)
             nc.vector.quantize_mx(out=codes[:].bitcast(FP8X4), scales=scale_bytes[:], in_=rounded[:])
             for t in range(2 * pairs):
-                w1_codes[g, 2 * a + t] = (codes[:, t * P : (t + 1) * P], scale_bytes[:, t * P : (t + 1) * P])
+                w1_tiles[g, 2 * first_pair + t] = (codes[:, t * P : (t + 1) * P], scale_bytes[:, t * P : (t + 1) * P])
 
         gather(x_scales, U8, picked_scales, 0, HALF, "picked_scales0")
         gather(x_scales, U8, picked_scales, HALF, HALF, "picked_scales1")
         gather(x_words[1], U32, picked_words[1], 0, HALF, "picked_words1")
-        quantise_w1(0, 0, 2, "w1_bf0")
-        gather(x_words[1], U32, picked_words[1], HALF, HALF // 2, "w1_bf0")
-        quantise_w1(1, 0, 1, "w1_bf1")
-        quantise_w1(1, 1, 1, "w1_bf2")
-        gather(x_words[1], U32, picked_words[1], HALF + HALF // 2, HALF // 2, "w1_bf2")
+        quantise_w1(0, 0, 2, "w1_pass0")
+        gather(x_words[1], U32, picked_words[1], HALF, QUARTER, "w1_pass0")
+        quantise_w1(1, 0, 1, "w1_pass1_pair0")
+        quantise_w1(1, 1, 1, "w1_pass1_pair1")
+        gather(x_words[1], U32, picked_words[1], HALF + QUARTER, QUARTER, "w1_pass1_pair1")
 
         sums = {}
         for first in range(0, S, GROUP):
             acc = psum.tile([P, PACK, GROUP], F32, name="acc", tag="bank")
-            for t in (0, 1, 2, 3) if first < 3 * GROUP else (2, 3, 0, 1):
+            for t in (0, 1, 2, 3) if first < EARLY_GROUPS * GROUP else (2, 3, 0, 1):
                 for g in range(PASSES):
                     words, word_cols = picked_words[g][first]
                     scale_rows, scale_cols = picked_scales[first]
                     nc.tensor.matmul_mx(
                         out=acc[:, t, :],
-                        lhsT=w1_codes[g, t][0].bitcast(FP8X4),
-                        lhsT_scale=w1_codes[g, t][1],
+                        lhsT=w1_tiles[g, t][0].bitcast(FP8X4),
+                        lhsT_scale=w1_tiles[g, t][1],
                         rhs=words[:, word_cols].bitcast(FP8X4),
                         rhs_scale=scale_rows[4 * g : P, scale_cols],
                         start=(g == 0),
@@ -146,28 +153,26 @@ def tile_picked_embpos_none_e_kernel(tc, xT, w1, w2_words, w2_scales, pos, offs,
                     )
             sums[first] = acc
 
-        def add_pos(h_bf, at, first):
-            u, within = divmod(first, HALF)
-            rounded = h_bf[:, at * PACK : (at + GROUP) * PACK]
-            place = pos_sb[u][:, :, within : within + GROUP]
-            if within == 0:
-                place_rows = keep.tile([P, GROUP * PACK], F32, name="place_rows")
-                nc.scalar.copy(out=place_rows[:].rearrange("p (c i t) -> p c t i", i=RUN, t=PACK), in_=place.rearrange("p t (c i) -> p c t i", i=RUN))
-                product = keep.tile([P, GROUP * PACK], F32, name="product%d" % first)
-                nc.scalar.copy(out=product[:].rearrange("p (n t) -> p n t", t=PACK), in_=sums[first][:].rearrange("p t n -> p n t"))
-                nc.gpsimd.tensor_tensor(out=rounded, in0=product[:], in1=place_rows[:], op=ADD)
-                return
-            nc.vector.tensor_tensor(
-                out=rounded.rearrange("p (c i t) -> p c t i", i=RUN, t=PACK),
-                in0=sums[first][:].rearrange("p t (c i) -> p c t i", i=RUN),
-                in1=place.rearrange("p t (c i) -> p c t i", i=RUN),
-                op=ADD,
-            )
+        def add_pos(first, rounded):
+            pos_pairs = pos_of[first].rearrange("p t (c i) -> p c t i", i=RUN)
+            if first == 0:
+                pos_laid = keep.tile([P, GROUP * PACK], F32, name="pos_laid")
+                nc.scalar.copy(out=pos_laid[:].rearrange("p (c i t) -> p c t i", i=RUN, t=PACK), in_=pos_pairs)
+                sum_laid = keep.tile([P, GROUP * PACK], F32, name="sum_laid")
+                nc.scalar.copy(out=sum_laid[:].rearrange("p (c t) -> p c t", t=PACK), in_=sums[first][:].rearrange("p t c -> p c t"))
+                nc.gpsimd.tensor_tensor(out=rounded, in0=sum_laid[:], in1=pos_laid[:], op=ADD)
+            else:
+                nc.vector.tensor_tensor(
+                    out=rounded.rearrange("p (c i t) -> p c t i", i=RUN, t=PACK),
+                    in0=sums[first][:].rearrange("p t (c i) -> p c t i", i=RUN),
+                    in1=pos_pairs,
+                    op=ADD,
+                )
 
-        def second_layer(h_bf, first, n):
+        def second_layer(first, n, rounded):
             h_codes = keep.tile([P, n], U32, name="h_codes%d" % first, align_bytes=64)
             h_bytes = keep.tile([P, n], U8, name="h_bytes%d" % first, align_bytes=64)
-            nc.vector.quantize_mx(out=h_codes[:].bitcast(FP8X4), scales=h_bytes[:], in_=h_bf[:])
+            nc.vector.quantize_mx(out=h_codes[:].bitcast(FP8X4), scales=h_bytes[:], in_=rounded)
             res = psum.tile([P, n], F32, name="res", tag="bank")
             nc.tensor.matmul_mx(
                 out=res[:],
@@ -182,14 +187,12 @@ def tile_picked_embpos_none_e_kernel(tc, xT, w1, w2_words, w2_scales, pos, offs,
             nc.scalar.copy(out=staged[:], in_=res[:])
             nc.sync.dma_start(out=out[:, first : first + n], in_=staged[:])
 
-        first = 0
-        for pieces in OUT_PIECES:
-            ready = []
-            for n in pieces:
-                h_bf = keep.tile([P, n * PACK], BF16, name="h_bf%d" % first, align_bytes=64)
-                for at in range(0, n, GROUP):
-                    add_pos(h_bf, at, first + at)
-                ready.append((h_bf, first, n))
-                first = first + n
-            for piece in ready:
-                second_layer(*piece)
+        entry = 0
+        for load, n in enumerate(POS_LOADS):
+            h_bf = keep.tile([P, n * PACK], BF16, name="h_bf", tag="h_bf%d" % (load % 2), align_bytes=64)
+            for at in range(0, n, GROUP):
+                add_pos(entry + at, h_bf[:, at * PACK : (at + GROUP) * PACK])
+            piece = GROUP if entry + n == S else n
+            for at in range(0, n, piece):
+                second_layer(entry + at, piece, h_bf[:, at * PACK : (at + piece) * PACK])
+            entry = entry + n

@@ -27,11 +27,14 @@ HALF = S // 2
 QUARTER = S // 4
 
 X_LOADS = (
-    (((512, 0), (0, 512)), ((0, 512), (512, 0))),
-    (((256, 256), (512, 0)), ((128, 384),), ((128, 128),), ((128, 128),)),
+    (((512, 0), (0, 512), (128, 128)), ((256, 256), (128, 128))),
+    (((512, 0), (0, 256)), ((256, 0), (128, 128), (0, 128)), ((192, 64), (0, 128)), ((160, 96),)),
 )
-POS_LOADS = (HALF, QUARTER, QUARTER)
-EARLY_GROUPS = 3
+POS_LOADS = (4 * GROUP, 3 * GROUP, GROUP)
+GPSIMD_GROUPS = 2
+EARLY_GROUPS = 4
+MATMUL_ORDER = (0, 2, 1, 3, 4, 5, 6, 7)
+H_TILES = (HALF, QUARTER, QUARTER)
 
 
 def tile_picked_embpos_none_e_kernel(tc, xT, w1, w2_words, w2_scales, pos, offs, out):
@@ -72,11 +75,11 @@ def tile_picked_embpos_none_e_kernel(tc, xT, w1, w2_words, w2_scales, pos, offs,
         pos_of = {}
         entry = 0
         for n in POS_LOADS:
-            raw = keep.tile([P, PACK, n], F32, name="pos%d" % entry)
+            raw = keep.tile([P, PACK, n], F32, name="pos", tag="pos%d" % entry, align_bytes=64)
             nc.sync.dma_start(out=raw[:], in_=pos_rows[:, :, entry : entry + n])
             for at in range(0, n, GROUP):
                 pos_of[entry + at] = raw[:, :, at : at + GROUP]
-            if entry == 0:
+            if entry + n == S:
                 nc.sync.dma_start(out=w2_codes[:].bitcast(I32), in_=w2_words[0].rearrange("p n t -> p (n t)").bitcast(I32))
                 for q in range(P // QUADRANT):
                     nc.sync.dma_start(
@@ -114,63 +117,67 @@ def tile_picked_embpos_none_e_kernel(tc, xT, w1, w2_words, w2_scales, pos, offs,
 
         w1_tiles = {}
 
-        def quantise_w1(g, first_pair, pairs, tag):
-            columns = pairs * 2 * P
-            rounded = keep.tile([P, columns * PACK], BF16, name="w1_bf", tag=tag, align_bytes=64)
-            dst = rounded[:].rearrange("p (a b m j) -> p a m j b", a=pairs, b=2, j=PACK)
+        def quantise_w1(g, pair, tag):
+            rounded = keep.tile([P, 2 * P * PACK], BF16, name="w1_bf", tag=tag, align_bytes=64)
+            dst = rounded[:].rearrange("p (b m j) -> p m j b", b=2, j=PACK)
             src = w1_raw[g][:].rearrange("p j (m a b) -> p a m j b", a=2, b=2)
-            nc.scalar.copy(out=dst, in_=src[:, first_pair : first_pair + pairs])
-            codes = keep.tile([P, columns], U32, name="w1_codes%d_%d" % (g, first_pair), align_bytes=64)
-            scale_bytes = keep.tile([P, columns], U8, name="w1_bytes%d_%d" % (g, first_pair), align_bytes=64)
+            nc.scalar.copy(out=dst, in_=src[:, pair])
+            codes = keep.tile([P, 2 * P], U32, name="w1_codes%d_%d" % (g, pair), align_bytes=64)
+            scale_bytes = keep.tile([P, 2 * P], U8, name="w1_bytes%d_%d" % (g, pair), align_bytes=64)
             nc.vector.quantize_mx(out=codes[:].bitcast(FP8X4), scales=scale_bytes[:], in_=rounded[:])
-            for t in range(2 * pairs):
-                w1_tiles[g, 2 * first_pair + t] = (codes[:, t * P : (t + 1) * P], scale_bytes[:, t * P : (t + 1) * P])
+            for b in range(2):
+                w1_tiles[g, 2 * pair + b] = (codes[:, b * P : (b + 1) * P], scale_bytes[:, b * P : (b + 1) * P])
 
         gather(x_scales, U8, picked_scales, 0, HALF, "picked_scales0")
-        gather(x_scales, U8, picked_scales, HALF, HALF, "picked_scales1")
         gather(x_words[1], U32, picked_words[1], 0, HALF, "picked_words1")
-        quantise_w1(0, 0, 2, "w1_pass0")
-        gather(x_words[1], U32, picked_words[1], HALF, QUARTER, "w1_pass0")
-        quantise_w1(1, 0, 1, "w1_pass1_pair0")
-        quantise_w1(1, 1, 1, "w1_pass1_pair1")
+        quantise_w1(0, 0, "w1_pass0_pair0")
+        gather(x_scales, U8, picked_scales, HALF, HALF, "w1_pass0_pair0")
+        quantise_w1(0, 1, "w1_pass0_pair1")
+        quantise_w1(1, 0, "w1_pass1_pair0")
+        gather(x_words[1], U32, picked_words[1], HALF, QUARTER, "w1_pass1_pair0")
+        quantise_w1(1, 1, "w1_pass1_pair1")
         gather(x_words[1], U32, picked_words[1], HALF + QUARTER, QUARTER, "w1_pass1_pair1")
 
         sums = {}
-        for first in range(0, S, GROUP):
+        for first in (GROUP * n for n in MATMUL_ORDER):
             acc = psum.tile([P, PACK, GROUP], F32, name="acc", tag="bank")
-            for t in (0, 1, 2, 3) if first < EARLY_GROUPS * GROUP else (2, 3, 0, 1):
-                for g in range(PASSES):
-                    words, word_cols = picked_words[g][first]
-                    scale_rows, scale_cols = picked_scales[first]
-                    nc.tensor.matmul_mx(
-                        out=acc[:, t, :],
-                        lhsT=w1_tiles[g, t][0].bitcast(FP8X4),
-                        lhsT_scale=w1_tiles[g, t][1],
-                        rhs=words[:, word_cols].bitcast(FP8X4),
-                        rhs_scale=scale_rows[4 * g : P, scale_cols],
-                        start=(g == 0),
-                        stop=(g == PASSES - 1),
-                    )
+            steps = [(g, t) for g in range(PASSES) for t in range(PACK)]
+            if first >= EARLY_GROUPS * GROUP:
+                steps = steps[::-1]
+            for g, t in steps:
+                words, word_cols = picked_words[g][first]
+                scale_rows, scale_cols = picked_scales[first]
+                nc.tensor.matmul_mx(
+                    out=acc[:, t, :],
+                    lhsT=w1_tiles[g, t][0].bitcast(FP8X4),
+                    lhsT_scale=w1_tiles[g, t][1],
+                    rhs=words[:, word_cols].bitcast(FP8X4),
+                    rhs_scale=scale_rows[4 * g : P, scale_cols],
+                    start=((g, t) == steps[0]),
+                    stop=((g, t) == steps[-1]),
+                )
             sums[first] = acc
 
         def add_pos(first, rounded):
-            pos_pairs = pos_of[first].rearrange("p t (c i) -> p c t i", i=RUN)
-            if first == 0:
-                pos_laid = keep.tile([P, GROUP * PACK], F32, name="pos_laid")
-                nc.scalar.copy(out=pos_laid[:].rearrange("p (c i t) -> p c t i", i=RUN, t=PACK), in_=pos_pairs)
-                sum_laid = keep.tile([P, GROUP * PACK], F32, name="sum_laid")
-                nc.scalar.copy(out=sum_laid[:].rearrange("p (c t) -> p c t", t=PACK), in_=sums[first][:].rearrange("p t c -> p c t"))
-                nc.gpsimd.tensor_tensor(out=rounded, in0=sum_laid[:], in1=pos_laid[:], op=ADD)
+            if first < GPSIMD_GROUPS * GROUP:
+                sum_laid = keep.tile([P, GROUP, PACK], F32, name="sum_laid%d" % first)
+                nc.scalar.copy(out=sum_laid[:], in_=sums[first][:].rearrange("p t c -> p c t"))
+                nc.gpsimd.tensor_tensor(
+                    out=rounded.rearrange("p (c t) -> p c t", t=PACK),
+                    in0=sum_laid[:],
+                    in1=pos_of[first].rearrange("p t c -> p c t"),
+                    op=ADD,
+                )
             else:
                 nc.vector.tensor_tensor(
                     out=rounded.rearrange("p (c i t) -> p c t i", i=RUN, t=PACK),
                     in0=sums[first][:].rearrange("p t (c i) -> p c t i", i=RUN),
-                    in1=pos_pairs,
+                    in1=pos_of[first].rearrange("p t (c i) -> p c t i", i=RUN),
                     op=ADD,
                 )
 
-        def second_layer(first, n, rounded):
-            h_codes = keep.tile([P, n], U32, name="h_codes%d" % first, align_bytes=64)
+        def second_layer(first, n, rounded, tag):
+            h_codes = keep.tile([P, n], U32, name="h_codes", tag=tag, align_bytes=64)
             h_bytes = keep.tile([P, n], U8, name="h_bytes%d" % first, align_bytes=64)
             nc.vector.quantize_mx(out=h_codes[:].bitcast(FP8X4), scales=h_bytes[:], in_=rounded)
             res = psum.tile([P, n], F32, name="res", tag="bank")
@@ -184,15 +191,23 @@ def tile_picked_embpos_none_e_kernel(tc, xT, w1, w2_words, w2_scales, pos, offs,
                 stop=True,
             )
             staged = keep.tile([P, n], F32, name="staged%d" % first)
-            nc.scalar.copy(out=staged[:], in_=res[:])
+            if first + n == S:
+                nc.vector.tensor_copy(out=staged[:], in_=res[:])
+            else:
+                nc.scalar.copy(out=staged[:], in_=res[:])
             nc.sync.dma_start(out=out[:, first : first + n], in_=staged[:])
 
-        entry = 0
-        for load, n in enumerate(POS_LOADS):
-            h_bf = keep.tile([P, n * PACK], BF16, name="h_bf", tag="h_bf%d" % (load % 2), align_bytes=64)
-            for at in range(0, n, GROUP):
-                add_pos(entry + at, h_bf[:, at * PACK : (at + GROUP) * PACK])
-            piece = GROUP if entry + n == S else n
-            for at in range(0, n, piece):
-                second_layer(entry + at, piece, h_bf[:, at * PACK : (at + piece) * PACK])
-            entry = entry + n
+        h_bf = [keep.tile([P, n * PACK], BF16, name="h_bf%d" % k, align_bytes=64) for k, n in enumerate(H_TILES)]
+        starts = [sum(H_TILES[:k]) for k in range(len(H_TILES))]
+
+        def add_group(first):
+            k = max(k for k in range(len(H_TILES)) if starts[k] <= first)
+            at = first - starts[k]
+            add_pos(first, h_bf[k][:, at * PACK : (at + GROUP) * PACK])
+
+        for first in range(0, S - GROUP, GROUP):
+            add_group(first)
+        second_layer(starts[0], H_TILES[0], h_bf[0][:], "pos%d" % POS_LOADS[0])
+        add_group(S - GROUP)
+        for k in range(1, len(H_TILES)):
+            second_layer(starts[k], H_TILES[k], h_bf[k][:], "h_codes%d" % k)

@@ -28,13 +28,13 @@ QUARTER = S // 4
 
 X_LOADS = (
     (((512, 0), (0, 512), (128, 128)), ((256, 256), (128, 128))),
-    (((512, 0), (0, 256)), ((256, 0), (128, 128), (0, 128)), ((192, 64), (0, 128)), ((160, 96),)),
+    (((512, 0),), ((256, 0), (128, 128)), ((128, 128), (128, 128)), ((128, 128),), ((128, 128),)),
 )
 POS_LOADS = (4 * GROUP, 3 * GROUP, GROUP)
 GPSIMD_GROUPS = 2
 EARLY_GROUPS = 4
 MATMUL_ORDER = (0, 2, 1, 3, 4, 5, 6, 7)
-H_TILES = (HALF, QUARTER, QUARTER)
+H_TILES = (HALF, QUARTER, GROUP, GROUP)
 
 
 def tile_picked_embpos_none_e_kernel(tc, xT, w1, w2_words, w2_scales, pos, offs, out):
@@ -79,7 +79,7 @@ def tile_picked_embpos_none_e_kernel(tc, xT, w1, w2_words, w2_scales, pos, offs,
             nc.sync.dma_start(out=raw[:], in_=pos_rows[:, :, entry : entry + n])
             for at in range(0, n, GROUP):
                 pos_of[entry + at] = raw[:, :, at : at + GROUP]
-            if entry + n == S:
+            if entry == POS_LOADS[0]:
                 nc.sync.dma_start(out=w2_codes[:].bitcast(I32), in_=w2_words[0].rearrange("p n t -> p (n t)").bitcast(I32))
                 for q in range(P // QUADRANT):
                     nc.sync.dma_start(
@@ -160,14 +160,14 @@ def tile_picked_embpos_none_e_kernel(tc, xT, w1, w2_words, w2_scales, pos, offs,
 
         def add_pos(first, rounded):
             if first < GPSIMD_GROUPS * GROUP:
-                sum_laid = keep.tile([P, GROUP, PACK], F32, name="sum_laid%d" % first)
-                nc.scalar.copy(out=sum_laid[:], in_=sums[first][:].rearrange("p t c -> p c t"))
-                nc.gpsimd.tensor_tensor(
-                    out=rounded.rearrange("p (c t) -> p c t", t=PACK),
-                    in0=sum_laid[:],
-                    in1=pos_of[first].rearrange("p t c -> p c t"),
-                    op=ADD,
+                pos_laid = keep.tile([P, GROUP * PACK], F32, name="pos_laid%d" % first)
+                nc.scalar.copy(
+                    out=pos_laid[:].rearrange("p (c i t) -> p c t i", i=RUN, t=PACK),
+                    in_=pos_of[first].rearrange("p t (c i) -> p c t i", i=RUN),
                 )
+                sum_laid = keep.tile([P, GROUP * PACK], F32, name="sum_laid%d" % first)
+                nc.scalar.copy(out=sum_laid[:].rearrange("p (c t) -> p c t", t=PACK), in_=sums[first][:].rearrange("p t c -> p c t"))
+                nc.gpsimd.tensor_tensor(out=rounded, in0=sum_laid[:], in1=pos_laid[:], op=ADD)
             else:
                 nc.vector.tensor_tensor(
                     out=rounded.rearrange("p (c i t) -> p c t i", i=RUN, t=PACK),
@@ -191,7 +191,7 @@ def tile_picked_embpos_none_e_kernel(tc, xT, w1, w2_words, w2_scales, pos, offs,
                 stop=True,
             )
             staged = keep.tile([P, n], F32, name="staged%d" % first)
-            if first + n == S:
+            if n == GROUP:
                 nc.vector.tensor_copy(out=staged[:], in_=res[:])
             else:
                 nc.scalar.copy(out=staged[:], in_=res[:])

@@ -30,10 +30,10 @@ X_LOADS = (
     (((512, 0), (0, 512), (128, 128)), ((256, 256), (128, 128))),
     (((512, 0),), ((256, 0), (128, 128)), ((128, 128), (128, 128)), ((128, 128),), ((128, 128),)),
 )
-POS_LOADS = (4 * GROUP, 3 * GROUP, GROUP)
-GPSIMD_GROUPS = 2
+POS_LOADS = (HALF, QUARTER, QUARTER)
+GPSIMD_GROUPS = 1
 EARLY_GROUPS = 4
-MATMUL_ORDER = (0, 2, 1, 3, 4, 5, 6, 7)
+MATMUL_ORDER = (0, 1, 2, 3, 4, 5, 6, 7)
 H_TILES = (HALF, QUARTER, GROUP, GROUP)
 
 
@@ -79,7 +79,7 @@ def tile_picked_embpos_none_e_kernel(tc, xT, w1, w2_words, w2_scales, pos, offs,
             nc.sync.dma_start(out=raw[:], in_=pos_rows[:, :, entry : entry + n])
             for at in range(0, n, GROUP):
                 pos_of[entry + at] = raw[:, :, at : at + GROUP]
-            if entry == POS_LOADS[0]:
+            if entry == 0:
                 nc.sync.dma_start(out=w2_codes[:].bitcast(I32), in_=w2_words[0].rearrange("p n t -> p (n t)").bitcast(I32))
                 for q in range(P // QUADRANT):
                     nc.sync.dma_start(
@@ -191,11 +191,9 @@ def tile_picked_embpos_none_e_kernel(tc, xT, w1, w2_words, w2_scales, pos, offs,
                 stop=True,
             )
             staged = keep.tile([P, n], F32, name="staged%d" % first)
-            if n == GROUP:
-                nc.vector.tensor_copy(out=staged[:], in_=res[:])
-            else:
-                nc.scalar.copy(out=staged[:], in_=res[:])
-            nc.sync.dma_start(out=out[:, first : first + n], in_=staged[:])
+            nc.scalar.copy(out=staged[:], in_=res[:])
+            queue = nc.scalar if first + n == S else nc.sync
+            queue.dma_start(out=out[:, first : first + n], in_=staged[:])
 
         h_bf = [keep.tile([P, n * PACK], BF16, name="h_bf%d" % k, align_bytes=64) for k, n in enumerate(H_TILES)]
         starts = [sum(H_TILES[:k]) for k in range(len(H_TILES))]
@@ -205,9 +203,12 @@ def tile_picked_embpos_none_e_kernel(tc, xT, w1, w2_words, w2_scales, pos, offs,
             at = first - starts[k]
             add_pos(first, h_bf[k][:, at * PACK : (at + GROUP) * PACK])
 
-        for first in range(0, S - GROUP, GROUP):
+        for first in range(0, 5 * GROUP, GROUP):
             add_group(first)
-        second_layer(starts[0], H_TILES[0], h_bf[0][:], "pos%d" % POS_LOADS[0])
-        add_group(S - GROUP)
-        for k in range(1, len(H_TILES)):
+        second_layer(starts[0], H_TILES[0], h_bf[0][:], "h_codes0")
+        add_group(5 * GROUP)
+        add_group(6 * GROUP)
+        second_layer(starts[1], H_TILES[1], h_bf[1][:], "h_codes1")
+        add_group(7 * GROUP)
+        for k in range(2, len(H_TILES)):
             second_layer(starts[k], H_TILES[k], h_bf[k][:], "h_codes%d" % k)

@@ -27,8 +27,8 @@ HALF = S // 2
 QUARTER = S // 4
 
 X_LOADS = (
-    (((512, 0), (0, 512), (128, 128)), ((256, 256), (128, 128))),
-    (((512, 0),), ((256, 0), (128, 128)), ((128, 128), (128, 128)), ((128, 128),), ((128, 128),)),
+    (((512, 0), (256, 0)), ((0, 256), (512, 0)), ((128, 128), (128, 128))),
+    (((512, 0),), ((512, 0),), ((128, 128), (128, 128)), ((128, 128),), ((128, 128),)),
 )
 POS_LOADS = (HALF, QUARTER, QUARTER)
 GPSIMD_GROUPS = 1

@@ -28,7 +28,7 @@ QUARTER = S // 4
 
 X_LOADS = (
     (((512, 0), (256, 0)), ((0, 256), (512, 0)), ((128, 128), (128, 128))),
-    (((512, 0),), ((512, 0),), ((128, 128), (128, 128)), ((128, 128),), ((128, 128),)),
+    (((512, 0),), ((256, 0), (192, 64)), ((128, 128), (128, 128)), ((128, 128),), ((128, 128),)),
 )
 POS_LOADS = (HALF, QUARTER, QUARTER)
 GPSIMD_GROUPS = 1
@@ -79,7 +79,7 @@ def tile_picked_embpos_none_e_kernel(tc, xT, w1, w2_words, w2_scales, pos, offs,
             nc.sync.dma_start(out=raw[:], in_=pos_rows[:, :, entry : entry + n])
             for at in range(0, n, GROUP):
                 pos_of[entry + at] = raw[:, :, at : at + GROUP]
-            if entry == 0:
+            if entry + n == S:
                 nc.sync.dma_start(out=w2_codes[:].bitcast(I32), in_=w2_words[0].rearrange("p n t -> p (n t)").bitcast(I32))
                 for q in range(P // QUADRANT):
                     nc.sync.dma_start(
@@ -203,12 +203,11 @@ def tile_picked_embpos_none_e_kernel(tc, xT, w1, w2_words, w2_scales, pos, offs,
             at = first - starts[k]
             add_pos(first, h_bf[k][:, at * PACK : (at + GROUP) * PACK])
 
-        for first in range(0, 5 * GROUP, GROUP):
+        for first in range(0, 6 * GROUP, GROUP):
             add_group(first)
-        second_layer(starts[0], H_TILES[0], h_bf[0][:], "h_codes0")
-        add_group(5 * GROUP)
+        for k in range(2):
+            second_layer(starts[k], H_TILES[k], h_bf[k][:], "h_codes%d" % k)
         add_group(6 * GROUP)
-        second_layer(starts[1], H_TILES[1], h_bf[1][:], "h_codes1")
         add_group(7 * GROUP)
         for k in range(2, len(H_TILES)):
             second_layer(starts[k], H_TILES[k], h_bf[k][:], "h_codes%d" % k)

@@ -27,7 +27,7 @@ HALF = S // 2
 QUARTER = S // 4
 
 X_LOADS = (
-    (((512, 0), (256, 0)), ((0, 256), (512, 0)), ((128, 128), (128, 128))),
+    (((256, 256), (512, 0)), ((0, 256), (256, 0)), ((128, 128), (128, 128))),
     (((512, 0),), ((256, 0), (192, 64)), ((128, 128), (128, 128)), ((128, 128),), ((128, 128),)),
 )
 POS_LOADS = (HALF, QUARTER, QUARTER)

@@ -26,14 +26,11 @@ GROUP = 128
 HALF = S // 2
 QUARTER = S // 4
 
-X_LOADS = (
-    (((256, 256), (512, 0)), ((0, 256), (256, 0)), ((128, 128), (128, 128))),
-    (((512, 0),), ((256, 0), (192, 64)), ((128, 128), (128, 128)), ((128, 128),), ((128, 128),)),
-)
-POS_LOADS = (HALF, QUARTER, QUARTER)
+ON_SCALAR = (512, 512, 768, 512, 1024, 512)
+POS_LOADS = (QUARTER, QUARTER, HALF)
 GPSIMD_GROUPS = 1
-EARLY_GROUPS = 4
-MATMUL_ORDER = (0, 1, 2, 3, 4, 5, 6, 7)
+EARLY_GROUPS = 3
+MATMUL_ORDER = (1, 0, 2, 3, 4, 5, 6, 7)
 H_TILES = (HALF, QUARTER, GROUP, GROUP)
 
 
@@ -44,26 +41,19 @@ def tile_picked_embpos_none_e_kernel(tc, xT, w1, w2_words, w2_scales, pos, offs,
         psum = ctx.enter_context(tc.psum_pool(name="psum", bufs=8))
 
         offsets = keep.tile([P, S // PER_COLUMN], U16, name="offsets")
-        x_words = [keep.tile([P, T], U32, name="x_words%d" % g, align_bytes=64) for g in range(PASSES)]
-        x_scales = keep.tile([P, T], U8, name="x_scales", align_bytes=64)
         w2_codes = keep.tile([P, N], U32, name="w2_codes", align_bytes=64)
         w2_bytes = keep.tile([P, N], U8, name="w2_bytes", align_bytes=64)
-
-        nc.gpsimd.memset(x_scales[:], 0)
         nc.gpsimd.memset(w2_bytes[:], 0)
 
-        x_raw = []
+        planes = []
         for g in range(PASSES):
             rows = xT[g * K_PASS : (g + 1) * K_PASS, :].rearrange("(p j) s -> p j s", j=PACK)
-            symbol = 0
-            for shares in X_LOADS[g]:
-                width = sum(on_scalar + on_vector for on_scalar, on_vector in shares)
-                raw = keep.tile([P, PACK, width], F32, name="x_raw%d_%d" % (g, symbol))
-                nc.sync.dma_start(out=raw[:], in_=rows[:, :, symbol : symbol + width])
-                if not x_raw:
+            for j in range(PACK):
+                plane = keep.tile([P, T], F32, name="plane%d_%d" % (g, j), align_bytes=64)
+                nc.sync.dma_start(out=plane[:], in_=rows[:, j, :])
+                if not planes:
                     nc.sync.dma_start(offsets[:], offs)
-                x_raw.append((g, symbol, raw, shares))
-                symbol = symbol + width
+                planes.append(plane)
 
         w1_raw = []
         for g in range(PASSES):
@@ -79,64 +69,94 @@ def tile_picked_embpos_none_e_kernel(tc, xT, w1, w2_words, w2_scales, pos, offs,
             nc.sync.dma_start(out=raw[:], in_=pos_rows[:, :, entry : entry + n])
             for at in range(0, n, GROUP):
                 pos_of[entry + at] = raw[:, :, at : at + GROUP]
-            if entry + n == S:
-                nc.sync.dma_start(out=w2_codes[:].bitcast(I32), in_=w2_words[0].rearrange("p n t -> p (n t)").bitcast(I32))
-                for q in range(P // QUADRANT):
-                    nc.sync.dma_start(
-                        out=w2_bytes[QUADRANT * q : QUADRANT * q + 4, :].bitcast(I32),
-                        in_=w2_scales[0][4 * q : 4 * q + 4, :].bitcast(I32),
-                    )
             entry = entry + n
+        nc.sync.dma_start(out=w2_codes[:].bitcast(I32), in_=w2_words[0].rearrange("p n t -> p (n t)").bitcast(I32))
+        for q in range(P // QUADRANT):
+            nc.sync.dma_start(
+                out=w2_bytes[QUADRANT * q : QUADRANT * q + 4, :].bitcast(I32),
+                in_=w2_scales[0][4 * q : 4 * q + 4, :].bitcast(I32),
+            )
 
-        picked_words = [{} for g in range(PASSES)]
-        picked_scales = {}
+        def gather(on_scalar, plane, dst, first, n):
+            picked = plane[:].indirect(offsets[:, first // PER_COLUMN : (first + n) // PER_COLUMN])
+            if on_scalar:
+                nc.scalar.activation(out=dst, in_=picked, func=COPY)
+            else:
+                nc.vector.tensor_copy(out=dst, in_=picked)
 
-        def gather(table, dtype, picked, first, n, tag):
-            tile = keep.tile([P, n], dtype, name="picked", tag=tag, align_bytes=64)
-            nc.vector.tensor_copy(tile[:], table[:].indirect(offsets[:, first // PER_COLUMN : (first + n) // PER_COLUMN]))
+        def weave(laid, u, pair):
+            nc.vector.tensor_copy(
+                out=laid[:].rearrange("p (c u e) -> p u c e", u=2, e=2)[:, u],
+                in_=pair.rearrange("p e c -> p c e"),
+            )
+
+        x_codes = [{} for g in range(PASSES)]
+
+        def quantise_x(g, first, n, laid):
+            codes = keep.tile([P, n], U32, name="x_codes%d_%d" % (g, first), align_bytes=64)
+            scale_bytes = keep.tile([P, n], U8, name="x_bytes%d_%d" % (g, first), align_bytes=64)
+            nc.vector.quantize_mx(out=codes[:].bitcast(FP8X4), scales=scale_bytes[:], in_=laid[:])
             for at in range(0, n, GROUP):
-                picked[first + at] = (tile, slice(at, at + GROUP))
+                x_codes[g][first + at] = (codes[:, at : at + GROUP], scale_bytes[:, at : at + GROUP])
 
-        for g, first, raw, shares in x_raw:
-            at = 0
-            for on_scalar, on_vector in shares:
-                n = on_scalar + on_vector
-                rounded = keep.tile([P, n * PACK], BF16, name="x_bf%d_%d" % (g, first + at), align_bytes=64)
-                dst = rounded[:].rearrange("p (c i j) -> p c j i", i=RUN, j=PACK)
-                src = raw[:, :, at : at + n].rearrange("p j (c i) -> p c j i", i=RUN)
-                cut = on_scalar // RUN
-                if on_scalar:
-                    nc.scalar.activation(out=dst[:, :cut], in_=src[:, :cut], func=COPY)
-                if on_vector:
-                    nc.vector.tensor_copy(out=dst[:, cut:], in_=src[:, cut:])
-                cols = slice(first + at, first + at + n)
-                nc.vector.quantize_mx(out=x_words[g][:, cols].bitcast(FP8X4), scales=x_scales[4 * g : P, cols], in_=rounded[:])
-                at = at + n
-            if g == 0 and first + at == T:
-                gather(x_words[0], U32, picked_words[0], 0, S, "picked_words0")
+        widths = (HALF, QUARTER)
+        laid = [
+            [keep.tile([P, widths[g] * PACK], BF16, name="laid%d_%d" % (g, first), align_bytes=64) for first in range(0, S, widths[g])]
+            for g in range(PASSES)
+        ]
+        for pair_number in range(3):
+            g, u = divmod(pair_number, 2)
+            pair = keep.tile([P, 2, S], BF16, name="pair%d" % pair_number, align_bytes=64)
+            for e in range(2):
+                cut = ON_SCALAR[2 * pair_number + e]
+                gather(True, planes[2 * pair_number + e], pair[:, e, :cut], 0, cut)
+                if cut < S:
+                    gather(False, planes[2 * pair_number + e], pair[:, e, cut:], cut, S - cut)
+            for c, tile in enumerate(laid[g]):
+                weave(tile, u, pair[:, :, c * widths[g] : (c + 1) * widths[g]])
+            if pair_number == 1:
+                for c, tile in enumerate(laid[0]):
+                    quantise_x(0, c * HALF, HALF, tile)
+
+        last = [keep.tile([P, 2, QUARTER], BF16, name="last%d" % c, align_bytes=64) for c in range(4)]
+        for e in range(2):
+            for c in range(4):
+                gather(c < 3, planes[6 + e], last[c][:, e, :], c * QUARTER, QUARTER)
+        order = (0, 3, 1, 2)
+        for n, c in enumerate(order):
+            weave(laid[1][c], 1, last[c][:])
+            if n > 0:
+                quantise_x(1, order[n - 1] * QUARTER, QUARTER, laid[1][order[n - 1]])
+        quantise_x(1, order[-1] * QUARTER, QUARTER, laid[1][order[-1]])
 
         w1_tiles = {}
+        w1_bf = {}
 
-        def quantise_w1(g, pair, tag):
-            rounded = keep.tile([P, 2 * P * PACK], BF16, name="w1_bf", tag=tag, align_bytes=64)
+        def round_w1(g, pair, cut):
+            rounded = keep.tile([P, 2 * P * PACK], BF16, name="w1_bf%d_%d" % (g, pair), align_bytes=64)
             dst = rounded[:].rearrange("p (b m j) -> p m j b", b=2, j=PACK)
             src = w1_raw[g][:].rearrange("p j (m a b) -> p a m j b", a=2, b=2)
-            nc.scalar.copy(out=dst, in_=src[:, pair])
+            if cut > 0:
+                nc.scalar.copy(out=dst[:, :cut], in_=src[:, pair, :cut])
+            if cut < P:
+                nc.vector.tensor_copy(out=dst[:, cut:], in_=src[:, pair, cut:])
+            w1_bf[g, pair] = rounded
+
+        def quantise_w1(g, pair):
             codes = keep.tile([P, 2 * P], U32, name="w1_codes%d_%d" % (g, pair), align_bytes=64)
             scale_bytes = keep.tile([P, 2 * P], U8, name="w1_bytes%d_%d" % (g, pair), align_bytes=64)
-            nc.vector.quantize_mx(out=codes[:].bitcast(FP8X4), scales=scale_bytes[:], in_=rounded[:])
+            nc.vector.quantize_mx(out=codes[:].bitcast(FP8X4), scales=scale_bytes[:], in_=w1_bf[g, pair][:])
             for b in range(2):
                 w1_tiles[g, 2 * pair + b] = (codes[:, b * P : (b + 1) * P], scale_bytes[:, b * P : (b + 1) * P])
 
-        gather(x_scales, U8, picked_scales, 0, HALF, "picked_scales0")
-        gather(x_words[1], U32, picked_words[1], 0, HALF, "picked_words1")
-        quantise_w1(0, 0, "w1_pass0_pair0")
-        gather(x_scales, U8, picked_scales, HALF, HALF, "w1_pass0_pair0")
-        quantise_w1(0, 1, "w1_pass0_pair1")
-        quantise_w1(1, 0, "w1_pass1_pair0")
-        gather(x_words[1], U32, picked_words[1], HALF, QUARTER, "w1_pass1_pair0")
-        quantise_w1(1, 1, "w1_pass1_pair1")
-        gather(x_words[1], U32, picked_words[1], HALF + QUARTER, QUARTER, "w1_pass1_pair1")
+        round_w1(0, 0, P)
+        quantise_w1(0, 0)
+        round_w1(0, 1, P // 2)
+        quantise_w1(0, 1)
+        round_w1(1, 0, 0)
+        round_w1(1, 1, 3 * P // 4)
+        quantise_w1(1, 0)
+        quantise_w1(1, 1)
 
         sums = {}
         for first in (GROUP * n for n in MATMUL_ORDER):
@@ -145,14 +165,12 @@ def tile_picked_embpos_none_e_kernel(tc, xT, w1, w2_words, w2_scales, pos, offs,
             if first >= EARLY_GROUPS * GROUP:
                 steps = steps[::-1]
             for g, t in steps:
-                words, word_cols = picked_words[g][first]
-                scale_rows, scale_cols = picked_scales[first]
                 nc.tensor.matmul_mx(
                     out=acc[:, t, :],
                     lhsT=w1_tiles[g, t][0].bitcast(FP8X4),
                     lhsT_scale=w1_tiles[g, t][1],
-                    rhs=words[:, word_cols].bitcast(FP8X4),
-                    rhs_scale=scale_rows[4 * g : P, scale_cols],
+                    rhs=x_codes[g][first][0].bitcast(FP8X4),
+                    rhs_scale=x_codes[g][first][1],
                     start=((g, t) == steps[0]),
                     stop=((g, t) == steps[-1]),
                 )

@@ -27,7 +27,7 @@ HALF = S // 2
 QUARTER = S // 4
 
 ON_SCALAR = (512, 512, 768, 512, 1024, 512)
-POS_LOADS = (QUARTER, QUARTER, HALF)
+POS_LOADS = (HALF, QUARTER, QUARTER)
 GPSIMD_GROUPS = 1
 EARLY_GROUPS = 3
 MATMUL_ORDER = (1, 0, 2, 3, 4, 5, 6, 7)
@@ -92,8 +92,8 @@ def tile_picked_embpos_none_e_kernel(tc, xT, w1, w2_words, w2_scales, pos, offs,
 
         x_codes = [{} for g in range(PASSES)]
 
-        def quantise_x(g, first, n, laid):
-            codes = keep.tile([P, n], U32, name="x_codes%d_%d" % (g, first), align_bytes=64)
+        def quantise_x(g, first, n, laid, tag):
+            codes = keep.tile([P, n], U32, name="x_codes", tag=tag, align_bytes=64)
             scale_bytes = keep.tile([P, n], U8, name="x_bytes%d_%d" % (g, first), align_bytes=64)
             nc.vector.quantize_mx(out=codes[:].bitcast(FP8X4), scales=scale_bytes[:], in_=laid[:])
             for at in range(0, n, GROUP):
@@ -116,24 +116,23 @@ def tile_picked_embpos_none_e_kernel(tc, xT, w1, w2_words, w2_scales, pos, offs,
                 weave(tile, u, pair[:, :, c * widths[g] : (c + 1) * widths[g]])
             if pair_number == 1:
                 for c, tile in enumerate(laid[0]):
-                    quantise_x(0, c * HALF, HALF, tile)
+                    quantise_x(0, c * HALF, HALF, tile, "x_codes0_%d" % c)
 
         last = [keep.tile([P, 2, QUARTER], BF16, name="last%d" % c, align_bytes=64) for c in range(4)]
         for e in range(2):
             for c in range(4):
                 gather(c < 3, planes[6 + e], last[c][:, e, :], c * QUARTER, QUARTER)
-        order = (0, 3, 1, 2)
-        for n, c in enumerate(order):
-            weave(laid[1][c], 1, last[c][:])
-            if n > 0:
-                quantise_x(1, order[n - 1] * QUARTER, QUARTER, laid[1][order[n - 1]])
-        quantise_x(1, order[-1] * QUARTER, QUARTER, laid[1][order[-1]])
+        weave(laid[1][0], 1, last[0][:])
+        weave(laid[1][1], 1, last[1][:])
+        quantise_x(1, 0, QUARTER, laid[1][0], "x_codes1_0")
+        weave(laid[1][2], 1, last[2][:])
+        nc.scalar.copy(out=laid[1][3][:].rearrange("p (c u e) -> p u c e", u=2, e=2)[:, 1], in_=last[3][:].rearrange("p e c -> p c e"))
 
         w1_tiles = {}
         w1_bf = {}
 
         def round_w1(g, pair, cut):
-            rounded = keep.tile([P, 2 * P * PACK], BF16, name="w1_bf%d_%d" % (g, pair), align_bytes=64)
+            rounded = keep.tile([P, 2 * P * PACK], BF16, name="w1_bf", tag="w1_bf%d_%d" % (g, pair), align_bytes=64)
             dst = rounded[:].rearrange("p (b m j) -> p m j b", b=2, j=PACK)
             src = w1_raw[g][:].rearrange("p j (m a b) -> p a m j b", a=2, b=2)
             if cut > 0:
@@ -149,14 +148,17 @@ def tile_picked_embpos_none_e_kernel(tc, xT, w1, w2_words, w2_scales, pos, offs,
             for b in range(2):
                 w1_tiles[g, 2 * pair + b] = (codes[:, b * P : (b + 1) * P], scale_bytes[:, b * P : (b + 1) * P])
 
-        round_w1(0, 0, P)
+        round_w1(0, 0, 0)
+        round_w1(0, 1, P)
         quantise_w1(0, 0)
-        round_w1(0, 1, P // 2)
+        quantise_x(1, QUARTER, QUARTER, laid[1][1], "w1_bf0_0")
         quantise_w1(0, 1)
         round_w1(1, 0, 0)
         round_w1(1, 1, 3 * P // 4)
         quantise_w1(1, 0)
         quantise_w1(1, 1)
+        quantise_x(1, 2 * QUARTER, QUARTER, laid[1][2], "w1_bf1_1")
+        quantise_x(1, 3 * QUARTER, QUARTER, laid[1][3], "w1_bf1_0")
 
         sums = {}
         for first in (GROUP * n for n in MATMUL_ORDER):

@@ -30,7 +30,7 @@ ON_SCALAR = (512, 512, 768, 512, 1024, 512)
 POS_LOADS = (HALF, QUARTER, QUARTER)
 GPSIMD_GROUPS = 1
 EARLY_GROUPS = 3
-MATMUL_ORDER = (1, 0, 2, 3, 4, 5, 6, 7)
+MATMUL_ORDER = (0, 1, 2, 3, 4, 5, 6, 7)
 H_TILES = (HALF, QUARTER, GROUP, GROUP)
 
 
@@ -180,14 +180,14 @@ def tile_picked_embpos_none_e_kernel(tc, xT, w1, w2_words, w2_scales, pos, offs,
 
         def add_pos(first, rounded):
             if first < GPSIMD_GROUPS * GROUP:
-                pos_laid = keep.tile([P, GROUP * PACK], F32, name="pos_laid%d" % first)
-                nc.scalar.copy(
-                    out=pos_laid[:].rearrange("p (c i t) -> p c t i", i=RUN, t=PACK),
-                    in_=pos_of[first].rearrange("p t (c i) -> p c t i", i=RUN),
-                )
                 sum_laid = keep.tile([P, GROUP * PACK], F32, name="sum_laid%d" % first)
                 nc.scalar.copy(out=sum_laid[:].rearrange("p (c t) -> p c t", t=PACK), in_=sums[first][:].rearrange("p t c -> p c t"))
-                nc.gpsimd.tensor_tensor(out=rounded, in0=sum_laid[:], in1=pos_laid[:], op=ADD)
+                nc.gpsimd.tensor_tensor(
+                    out=rounded.rearrange("p (c t) -> p c t", t=PACK),
+                    in0=sum_laid[:].rearrange("p (c t) -> p c t", t=PACK),
+                    in1=pos_of[first].rearrange("p t c -> p c t"),
+                    op=ADD,
+                )
             else:
                 nc.vector.tensor_tensor(
                     out=rounded.rearrange("p (c i t) -> p c t i", i=RUN, t=PACK),

@@ -70,12 +70,13 @@ def tile_picked_embpos_none_e_kernel(tc, xT, w1, w2_words, w2_scales, pos, offs,
             for at in range(0, n, GROUP):
                 pos_of[entry + at] = raw[:, :, at : at + GROUP]
             entry = entry + n
-        nc.sync.dma_start(out=w2_codes[:].bitcast(I32), in_=w2_words[0].rearrange("p n t -> p (n t)").bitcast(I32))
-        for q in range(P // QUADRANT):
-            nc.sync.dma_start(
-                out=w2_bytes[QUADRANT * q : QUADRANT * q + 4, :].bitcast(I32),
-                in_=w2_scales[0][4 * q : 4 * q + 4, :].bitcast(I32),
-            )
+            if entry == S - POS_LOADS[-1]:
+                nc.sync.dma_start(out=w2_codes[:].bitcast(I32), in_=w2_words[0].rearrange("p n t -> p (n t)").bitcast(I32))
+                for q in range(P // QUADRANT):
+                    nc.sync.dma_start(
+                        out=w2_bytes[QUADRANT * q : QUADRANT * q + 4, :].bitcast(I32),
+                        in_=w2_scales[0][4 * q : 4 * q + 4, :].bitcast(I32),
+                    )
 
         def gather(on_scalar, plane, dst, first, n):
             picked = plane[:].indirect(offsets[:, first // PER_COLUMN : (first + n) // PER_COLUMN])

@@ -30,7 +30,7 @@ ON_SCALAR = (512, 512, 768, 512, 1024, 512)
 POS_LOADS = (HALF, QUARTER, QUARTER)
 GPSIMD_GROUPS = 1
 EARLY_GROUPS = 3
-MATMUL_ORDER = (0, 1, 2, 3, 4, 5, 6, 7)
+MATMUL_ORDER = (1, 0, 2, 3, 4, 5, 6, 7)
 H_TILES = (HALF, QUARTER, GROUP, GROUP)
 
 

@@ -213,8 +213,7 @@ def tile_picked_embpos_none_e_kernel(tc, xT, w1, w2_words, w2_scales, pos, offs,
             )
             staged = keep.tile([P, n], F32, name="staged%d" % first)
             nc.scalar.copy(out=staged[:], in_=res[:])
-            queue = nc.scalar if first + n == S else nc.sync
-            queue.dma_start(out=out[:, first : first + n], in_=staged[:])
+            nc.sync.dma_start(out=out[:, first : first + n], in_=staged[:])
 
         h_bf = [keep.tile([P, n * PACK], BF16, name="h_bf%d" % k, align_bytes=64) for k, n in enumerate(H_TILES)]
         starts = [sum(H_TILES[:k]) for k in range(len(H_TILES))]

@@ -29,6 +29,7 @@ QUARTER = S // 4
 ON_SCALAR = (512, 512, 768, 512, 1024, 512)
 POS_LOADS = (HALF, QUARTER, QUARTER)
 GPSIMD_GROUPS = 1
+WARM_UPS = 7
 EARLY_GROUPS = 3
 MATMUL_ORDER = (1, 0, 2, 3, 4, 5, 6, 7)
 H_TILES = (HALF, QUARTER, GROUP, GROUP)
@@ -161,6 +162,18 @@ def tile_picked_embpos_none_e_kernel(tc, xT, w1, w2_words, w2_scales, pos, offs,
         quantise_x(1, 2 * QUARTER, QUARTER, laid[1][2], "w1_bf1_1")
         quantise_x(1, 3 * QUARTER, QUARTER, laid[1][3], "w1_bf1_0")
 
+        warm = psum.tile([P, PACK, GROUP], F32, name="warm", tag="bank")
+        for n in range(WARM_UPS):
+            codes, scale_bytes = x_codes[1][0]
+            nc.tensor.matmul_mx(
+                out=warm[:, n % PACK, :],
+                lhsT=codes.bitcast(FP8X4),
+                lhsT_scale=scale_bytes,
+                rhs=codes.bitcast(FP8X4),
+                rhs_scale=scale_bytes,
+                start=True,
+                stop=True,
+            )
         sums = {}
         for first in (GROUP * n for n in MATMUL_ORDER):
             acc = psum.tile([P, PACK, GROUP], F32, name="acc", tag="bank")

@@ -26,7 +26,9 @@ GROUP = 128
 HALF = S // 2
 QUARTER = S // 4
 
-ON_SCALAR = (512, 512, 768, 512, 1024, 512)
+ON_SCALAR = (512, 512, 768, 512)
+PIECES = (QUARTER, QUARTER, QUARTER, GROUP, GROUP)
+ON_VECTOR = ((), (2, 3, 4), (0,), (0,))
 POS_LOADS = (HALF, QUARTER, QUARTER)
 GPSIMD_GROUPS = 1
 WARM_UPS = 7
@@ -58,7 +60,7 @@ def tile_picked_embpos_none_e_kernel(tc, xT, w1, w2_words, w2_scales, pos, offs,
 
         w1_raw = []
         for g in range(PASSES):
-            raw = keep.tile([P, PACK, H], F32, name="w1_raw%d" % g)
+            raw = keep.tile([P, PACK, H], F32, name="w1_raw", tag="w1_raw%d" % g, align_bytes=64)
             nc.sync.dma_start(out=raw[:], in_=w1[g * K_PASS : (g + 1) * K_PASS, :].rearrange("(p j) i -> p j i", j=PACK))
             w1_raw.append(raw)
 
@@ -86,8 +88,8 @@ def tile_picked_embpos_none_e_kernel(tc, xT, w1, w2_words, w2_scales, pos, offs,
             else:
                 nc.vector.tensor_copy(out=dst, in_=picked)
 
-        def weave(laid, u, pair):
-            nc.vector.tensor_copy(
+        def weave(copy, laid, u, pair):
+            copy(
                 out=laid[:].rearrange("p (c u e) -> p u c e", u=2, e=2)[:, u],
                 in_=pair.rearrange("p e c -> p c e"),
             )
@@ -101,34 +103,37 @@ def tile_picked_embpos_none_e_kernel(tc, xT, w1, w2_words, w2_scales, pos, offs,
             for at in range(0, n, GROUP):
                 x_codes[g][first + at] = (codes[:, at : at + GROUP], scale_bytes[:, at : at + GROUP])
 
-        widths = (HALF, QUARTER)
+        starts_x = [sum(PIECES[:c]) for c in range(len(PIECES))]
         laid = [
-            [keep.tile([P, widths[g] * PACK], BF16, name="laid%d_%d" % (g, first), align_bytes=64) for first in range(0, S, widths[g])]
-            for g in range(PASSES)
+            [keep.tile([P, n * PACK], BF16, name="laid", tag="laid%d_%d" % (g, c), align_bytes=64) for c, n in enumerate(widths)]
+            for g, widths in enumerate(((HALF, HALF), (QUARTER, QUARTER, QUARTER + GROUP)))
         ]
-        for pair_number in range(3):
-            g, u = divmod(pair_number, 2)
-            pair = keep.tile([P, 2, S], BF16, name="pair%d" % pair_number, align_bytes=64)
+        late = laid[1][2]
+        laid[1][2:] = [late[:, : QUARTER * PACK], late[:, QUARTER * PACK :]]
+        for u in range(2):
+            pair = keep.tile([P, 2, S], BF16, name="pair%d" % u, align_bytes=64)
             for e in range(2):
-                cut = ON_SCALAR[2 * pair_number + e]
-                gather(True, planes[2 * pair_number + e], pair[:, e, :cut], 0, cut)
-                if cut < S:
-                    gather(False, planes[2 * pair_number + e], pair[:, e, cut:], cut, S - cut)
-            for c, tile in enumerate(laid[g]):
-                weave(tile, u, pair[:, :, c * widths[g] : (c + 1) * widths[g]])
-            if pair_number == 1:
-                for c, tile in enumerate(laid[0]):
-                    quantise_x(0, c * HALF, HALF, tile, "x_codes0_%d" % c)
+                cut = ON_SCALAR[2 * u + e]
+                gather(True, planes[2 * u + e], pair[:, e, :cut], 0, cut)
+                gather(False, planes[2 * u + e], pair[:, e, cut:], cut, S - cut)
+            for c, tile in enumerate(laid[0]):
+                weave(nc.vector.tensor_copy, tile, u, pair[:, :, c * HALF : (c + 1) * HALF])
+        for c, tile in enumerate(laid[0]):
+            quantise_x(0, c * HALF, HALF, tile, "x_codes0_%d" % c)
 
-        last = [keep.tile([P, 2, QUARTER], BF16, name="last%d" % c, align_bytes=64) for c in range(4)]
-        for e in range(2):
-            for c in range(4):
-                gather(c < 3, planes[6 + e], last[c][:, e, :], c * QUARTER, QUARTER)
-        weave(laid[1][0], 1, last[0][:])
-        weave(laid[1][1], 1, last[1][:])
+        picked = [keep.tile([P, PACK, n], BF16, name="picked%d" % c, align_bytes=64) for c, n in enumerate(PIECES)]
+        for j in range(PACK):
+            for c, n in enumerate(PIECES):
+                gather(c not in ON_VECTOR[j], planes[PACK + j], picked[c][:, j, :], starts_x[c], n)
+            if j == 1:
+                for c in range(len(PIECES) - 1):
+                    weave(nc.vector.tensor_copy, laid[1][c], 0, picked[c][:, :2])
+
+        weave(nc.vector.tensor_copy, laid[1][0], 1, picked[0][:, 2:])
+        weave(nc.vector.tensor_copy, laid[1][1], 1, picked[1][:, 2:])
+        weave(nc.vector.tensor_copy, laid[1][2], 1, picked[2][:, 2:])
         quantise_x(1, 0, QUARTER, laid[1][0], "x_codes1_0")
-        weave(laid[1][2], 1, last[2][:])
-        nc.scalar.copy(out=laid[1][3][:].rearrange("p (c u e) -> p u c e", u=2, e=2)[:, 1], in_=last[3][:].rearrange("p e c -> p c e"))
+        weave(nc.scalar.copy, laid[1][3], 1, picked[3][:, 2:])
 
         w1_tiles = {}
         w1_bf = {}
@@ -146,21 +151,29 @@ def tile_picked_embpos_none_e_kernel(tc, xT, w1, w2_words, w2_scales, pos, offs,
         def quantise_w1(g, pair):
             codes = keep.tile([P, 2 * P], U32, name="w1_codes%d_%d" % (g, pair), align_bytes=64)
             scale_bytes = keep.tile([P, 2 * P], U8, name="w1_bytes%d_%d" % (g, pair), align_bytes=64)
-            nc.vector.quantize_mx(out=codes[:].bitcast(FP8X4), scales=scale_bytes[:], in_=w1_bf[g, pair][:])
+            step = P if (g, pair) == (0, 0) else 2 * P
+            for at in range(0, 2 * P, step):
+                nc.vector.quantize_mx(
+                    out=codes[:, at : at + step].bitcast(FP8X4),
+                    scales=scale_bytes[:, at : at + step],
+                    in_=w1_bf[g, pair][:, at * PACK : (at + step) * PACK],
+                )
             for b in range(2):
                 w1_tiles[g, 2 * pair + b] = (codes[:, b * P : (b + 1) * P], scale_bytes[:, b * P : (b + 1) * P])
 
         round_w1(0, 0, 0)
-        round_w1(0, 1, P)
+        round_w1(0, 1, 3 * P // 4)
+        laid_last = keep.tile([P, GROUP * PACK], BF16, name="laid_last", tag="w1_raw0", align_bytes=64)
+        nc.scalar.copy(out=laid_last[:].rearrange("p (c j) -> p c j", j=PACK), in_=picked[4][:].rearrange("p j c -> p c j"))
         quantise_w1(0, 0)
-        quantise_x(1, QUARTER, QUARTER, laid[1][1], "w1_bf0_0")
         quantise_w1(0, 1)
+        quantise_x(1, QUARTER, QUARTER, laid[1][1], "w1_bf0_0")
         round_w1(1, 0, 0)
-        round_w1(1, 1, 3 * P // 4)
+        round_w1(1, 1, 11 * P // 16)
         quantise_w1(1, 0)
         quantise_w1(1, 1)
-        quantise_x(1, 2 * QUARTER, QUARTER, laid[1][2], "w1_bf1_1")
-        quantise_x(1, 3 * QUARTER, QUARTER, laid[1][3], "w1_bf1_0")
+        quantise_x(1, starts_x[2], QUARTER + GROUP, late, "w1_bf1_0")
+        quantise_x(1, starts_x[4], PIECES[4], laid_last, "w1_bf1_1")
 
         warm = psum.tile([P, PACK, GROUP], F32, name="warm", tag="bank")
         for n in range(WARM_UPS):

@@ -162,14 +162,14 @@ def tile_picked_embpos_none_e_kernel(tc, xT, w1, w2_words, w2_scales, pos, offs,
                 w1_tiles[g, 2 * pair + b] = (codes[:, b * P : (b + 1) * P], scale_bytes[:, b * P : (b + 1) * P])
 
         round_w1(0, 0, 0)
-        round_w1(0, 1, 3 * P // 4)
+        round_w1(0, 1, 5 * P // 8)
         laid_last = keep.tile([P, GROUP * PACK], BF16, name="laid_last", tag="w1_raw0", align_bytes=64)
         nc.scalar.copy(out=laid_last[:].rearrange("p (c j) -> p c j", j=PACK), in_=picked[4][:].rearrange("p j c -> p c j"))
         quantise_w1(0, 0)
         quantise_w1(0, 1)
         quantise_x(1, QUARTER, QUARTER, laid[1][1], "w1_bf0_0")
         round_w1(1, 0, 0)
-        round_w1(1, 1, 11 * P // 16)
+        round_w1(1, 1, 5 * P // 8)
         quantise_w1(1, 0)
         quantise_w1(1, 1)
         quantise_x(1, starts_x[2], QUARTER + GROUP, late, "w1_bf1_0")
@@ -223,7 +223,7 @@ def tile_picked_embpos_none_e_kernel(tc, xT, w1, w2_words, w2_scales, pos, offs,
                     op=ADD,
                 )
 
-        def second_layer(first, n, rounded, tag):
+        def second_layer(first, n, rounded, tag, staged):
             h_codes = keep.tile([P, n], U32, name="h_codes", tag=tag, align_bytes=64)
             h_bytes = keep.tile([P, n], U8, name="h_bytes%d" % first, align_bytes=64)
             nc.vector.quantize_mx(out=h_codes[:].bitcast(FP8X4), scales=h_bytes[:], in_=rounded)
@@ -237,9 +237,7 @@ def tile_picked_embpos_none_e_kernel(tc, xT, w1, w2_words, w2_scales, pos, offs,
                 start=True,
                 stop=True,
             )
-            staged = keep.tile([P, n], F32, name="staged%d" % first)
-            nc.scalar.copy(out=staged[:], in_=res[:])
-            nc.sync.dma_start(out=out[:, first : first + n], in_=staged[:])
+            nc.scalar.copy(out=staged, in_=res[:])
 
         h_bf = [keep.tile([P, n * PACK], BF16, name="h_bf%d" % k, align_bytes=64) for k, n in enumerate(H_TILES)]
         starts = [sum(H_TILES[:k]) for k in range(len(H_TILES))]
@@ -252,8 +250,13 @@ def tile_picked_embpos_none_e_kernel(tc, xT, w1, w2_words, w2_scales, pos, offs,
         for first in range(0, 6 * GROUP, GROUP):
             add_group(first)
         for k in range(2):
-            second_layer(starts[k], H_TILES[k], h_bf[k][:], "h_codes%d" % k)
+            staged = keep.tile([P, H_TILES[k]], F32, name="staged%d" % k)
+            second_layer(starts[k], H_TILES[k], h_bf[k][:], "h_codes%d" % k, staged[:])
+            nc.sync.dma_start(out=out[:, starts[k] : starts[k + 1]], in_=staged[:])
         add_group(6 * GROUP)
         add_group(7 * GROUP)
+        staged = keep.tile([P, S - starts[2]], F32, name="staged2")
         for k in range(2, len(H_TILES)):
-            second_layer(starts[k], H_TILES[k], h_bf[k][:], "h_codes%d" % k)
+            at = starts[k] - starts[2]
+            second_layer(starts[k], H_TILES[k], h_bf[k][:], "h_codes%d" % k, staged[:, at : at + H_TILES[k]])
+        nc.sync.dma_start(out=out[:, starts[2] :], in_=staged[:])

@@ -29,11 +29,7 @@ QUARTER = S // 4
 ON_SCALAR = (512, 512, 768, 512)
 PIECES = (QUARTER, QUARTER, QUARTER, GROUP, GROUP)
 ON_VECTOR = ((), (2, 3, 4), (0,), (0,))
-POS_LOADS = (HALF, QUARTER, QUARTER)
-GPSIMD_GROUPS = 1
 WARM_UPS = 7
-EARLY_GROUPS = 3
-MATMUL_ORDER = (1, 0, 2, 3, 4, 5, 6, 7)
 H_TILES = (HALF, QUARTER, GROUP, GROUP)
 
 
@@ -65,15 +61,18 @@ def tile_picked_embpos_none_e_kernel(tc, xT, w1, w2_words, w2_scales, pos, offs,
             w1_raw.append(raw)
 
         pos_rows = pos.rearrange("(p t) s -> p t s", t=PACK)
+        pos_pairs = []
+        for u in range(2):
+            raw = keep.tile([P, 2, HALF], F32, name="pos_pair%d" % u, align_bytes=64)
+            nc.sync.dma_start(out=raw[:], in_=pos_rows[:, 2 * u : 2 * u + 2, :HALF])
+            pos_pairs.append(raw)
         pos_of = {}
-        entry = 0
-        for n in POS_LOADS:
-            raw = keep.tile([P, PACK, n], F32, name="pos", tag="pos%d" % entry, align_bytes=64)
-            nc.sync.dma_start(out=raw[:], in_=pos_rows[:, :, entry : entry + n])
-            for at in range(0, n, GROUP):
+        for entry in range(HALF, S, QUARTER):
+            raw = keep.tile([P, PACK, QUARTER], F32, name="pos%d" % entry, align_bytes=64)
+            nc.sync.dma_start(out=raw[:], in_=pos_rows[:, :, entry : entry + QUARTER])
+            for at in range(0, QUARTER, GROUP):
                 pos_of[entry + at] = raw[:, :, at : at + GROUP]
-            entry = entry + n
-            if entry == S - POS_LOADS[-1]:
+            if entry == HALF:
                 nc.sync.dma_start(out=w2_codes[:].bitcast(I32), in_=w2_words[0].rearrange("p n t -> p (n t)").bitcast(I32))
                 for q in range(P // QUADRANT):
                     nc.sync.dma_start(
@@ -101,7 +100,7 @@ def tile_picked_embpos_none_e_kernel(tc, xT, w1, w2_words, w2_scales, pos, offs,
             scale_bytes = keep.tile([P, n], U8, name="x_bytes%d_%d" % (g, first), align_bytes=64)
             nc.vector.quantize_mx(out=codes[:].bitcast(FP8X4), scales=scale_bytes[:], in_=laid[:])
             for at in range(0, n, GROUP):
-                x_codes[g][first + at] = (codes[:, at : at + GROUP], scale_bytes[:, at : at + GROUP])
+                x_codes[g][first + at] = (codes[:, at:], scale_bytes[:, at:])
 
         starts_x = [sum(PIECES[:c]) for c in range(len(PIECES))]
         laid = [
@@ -177,7 +176,7 @@ def tile_picked_embpos_none_e_kernel(tc, xT, w1, w2_words, w2_scales, pos, offs,
 
         warm = psum.tile([P, PACK, GROUP], F32, name="warm", tag="bank")
         for n in range(WARM_UPS):
-            codes, scale_bytes = x_codes[1][0]
+            codes, scale_bytes = (part[:, :GROUP] for part in x_codes[1][0])
             nc.tensor.matmul_mx(
                 out=warm[:, n % PACK, :],
                 lhsT=codes.bitcast(FP8X4),
@@ -187,41 +186,56 @@ def tile_picked_embpos_none_e_kernel(tc, xT, w1, w2_words, w2_scales, pos, offs,
                 start=True,
                 stop=True,
             )
-        sums = {}
-        for first in (GROUP * n for n in MATMUL_ORDER):
-            acc = psum.tile([P, PACK, GROUP], F32, name="acc", tag="bank")
-            steps = [(g, t) for g in range(PASSES) for t in range(PACK)]
-            if first >= EARLY_GROUPS * GROUP:
-                steps = steps[::-1]
+        def first_layer(first, n, steps):
+            low = min(t for g, t in steps)
+            acc = psum.tile([P, len(steps) // PASSES, n], F32, name="acc", tag="bank")
             for g, t in steps:
                 nc.tensor.matmul_mx(
-                    out=acc[:, t, :],
+                    out=acc[:, t - low, :],
                     lhsT=w1_tiles[g, t][0].bitcast(FP8X4),
                     lhsT_scale=w1_tiles[g, t][1],
-                    rhs=x_codes[g][first][0].bitcast(FP8X4),
-                    rhs_scale=x_codes[g][first][1],
+                    rhs=x_codes[g][first][0][:, :n].bitcast(FP8X4),
+                    rhs_scale=x_codes[g][first][1][:, :n],
                     start=((g, t) == steps[0]),
                     stop=((g, t) == steps[-1]),
                 )
-            sums[first] = acc
+            return acc
 
-        def add_pos(first, rounded):
-            if first < GPSIMD_GROUPS * GROUP:
-                sum_laid = keep.tile([P, GROUP * PACK], F32, name="sum_laid%d" % first)
-                nc.scalar.copy(out=sum_laid[:].rearrange("p (c t) -> p c t", t=PACK), in_=sums[first][:].rearrange("p t c -> p c t"))
+        pair_sums = {}
+        for u in range(2):
+            for first in (0, QUARTER) if u == 0 else (QUARTER, 0):
+                steps = [(g, 2 * u + e) for g in range(PASSES) for e in range(2)]
+                pair_sums[first, u] = first_layer(first, QUARTER, steps[::-1] if (first, u) == (0, 1) else steps)
+        sums = {}
+        for first in range(HALF, S, GROUP):
+            sums[first] = first_layer(first, GROUP, [(g, t) for g in range(PASSES) for t in range(PACK)][::-1])
+
+        def add_pair(first, u, rounded):
+            pos_part = pos_pairs[u][:, :, first : first + QUARTER]
+            if (first, u) == (QUARTER, 0):
+                sum_laid = keep.tile([P, 2 * QUARTER], F32, name="sum_laid")
+                nc.scalar.copy(out=sum_laid[:].rearrange("p (c e) -> p c e", e=2), in_=pair_sums[first, u][:].rearrange("p e c -> p c e"))
                 nc.gpsimd.tensor_tensor(
-                    out=rounded.rearrange("p (c t) -> p c t", t=PACK),
-                    in0=sum_laid[:].rearrange("p (c t) -> p c t", t=PACK),
-                    in1=pos_of[first].rearrange("p t c -> p c t"),
+                    out=rounded,
+                    in0=sum_laid[:].rearrange("p (c e) -> p c e", e=2),
+                    in1=pos_part.rearrange("p e c -> p c e"),
                     op=ADD,
                 )
             else:
                 nc.vector.tensor_tensor(
-                    out=rounded.rearrange("p (c i t) -> p c t i", i=RUN, t=PACK),
-                    in0=sums[first][:].rearrange("p t (c i) -> p c t i", i=RUN),
-                    in1=pos_of[first].rearrange("p t (c i) -> p c t i", i=RUN),
+                    out=rounded.rearrange("p (c i e) -> p c e i", i=RUN, e=2),
+                    in0=pair_sums[first, u][:].rearrange("p e (c i) -> p c e i", i=RUN),
+                    in1=pos_part.rearrange("p e (c i) -> p c e i", i=RUN),
                     op=ADD,
                 )
+
+        def add_pos(first, rounded):
+            nc.vector.tensor_tensor(
+                out=rounded.rearrange("p (c i t) -> p c t i", i=RUN, t=PACK),
+                in0=sums[first][:].rearrange("p t (c i) -> p c t i", i=RUN),
+                in1=pos_of[first].rearrange("p t (c i) -> p c t i", i=RUN),
+                op=ADD,
+            )
 
         def second_layer(first, n, rounded, tag, staged):
             h_codes = keep.tile([P, n], U32, name="h_codes", tag=tag, align_bytes=64)
@@ -247,7 +261,19 @@ def tile_picked_embpos_none_e_kernel(tc, xT, w1, w2_words, w2_scales, pos, offs,
             at = first - starts[k]
             add_pos(first, h_bf[k][:, at * PACK : (at + GROUP) * PACK])
 
-        for first in range(0, 6 * GROUP, GROUP):
+        h_words = h_bf[0][:].bitcast(U32).rearrange("p (c u) -> p c u", u=2)
+        both = keep.tile([P, 2, 2 * QUARTER], BF16, name="h_pairs", align_bytes=64)
+        upper = keep.tile([P, 2 * QUARTER], BF16, name="h_upper", align_bytes=64)
+        add_pair(0, 0, both[:, 0, :])
+        add_pair(QUARTER, 0, h_bf[0][:].rearrange("p (c u e) -> p u c e", u=2, e=2)[:, 0, QUARTER:])
+        add_pair(QUARTER, 1, upper[:])
+        add_pair(0, 1, both[:, 1, :])
+        nc.scalar.copy(out=h_words[:, QUARTER:, 1], in_=upper[:].bitcast(U32))
+        nc.scalar.copy(
+            out=h_words[:, :QUARTER],
+            in_=both[:].rearrange("p u w -> p (u w)").bitcast(U32).rearrange("p (u c) -> p c u", u=2),
+        )
+        for first in range(HALF, 6 * GROUP, GROUP):
             add_group(first)
         for k in range(2):
             staged = keep.tile([P, H_TILES[k]], F32, name="staged%d" % k)

@@ -27,10 +27,10 @@ HALF = S // 2
 QUARTER = S // 4
 
 ON_SCALAR = (512, 512, 768, 512)
-PIECES = (QUARTER, QUARTER, QUARTER, GROUP, GROUP)
-ON_VECTOR = ((), (2, 3, 4), (0,), (0,))
+ON_VECTOR = ((), (2, 3), (0,), (0,))
 WARM_UPS = 7
-H_TILES = (HALF, QUARTER, GROUP, GROUP)
+H_TILES = (3 * GROUP, 3 * GROUP, GROUP, GROUP)
+ON_GPSIMD = 3 * GROUP
 
 
 def tile_picked_embpos_none_e_kernel(tc, xT, w1, w2_words, w2_scales, pos, offs, out):
@@ -61,12 +61,10 @@ def tile_picked_embpos_none_e_kernel(tc, xT, w1, w2_words, w2_scales, pos, offs,
             w1_raw.append(raw)
 
         pos_rows = pos.rearrange("(p t) s -> p t s", t=PACK)
-        pos_pairs = []
+        pos_first = keep.tile([P, PACK, HALF], F32, name="pos_first", align_bytes=64)
         for u in range(2):
-            raw = keep.tile([P, 2, HALF], F32, name="pos_pair%d" % u, align_bytes=64)
-            nc.sync.dma_start(out=raw[:], in_=pos_rows[:, 2 * u : 2 * u + 2, :HALF])
-            pos_pairs.append(raw)
-        pos_of = {}
+            nc.sync.dma_start(out=pos_first[:, 2 * u : 2 * u + 2, :], in_=pos_rows[:, 2 * u : 2 * u + 2, :HALF])
+        pos_of = {first: pos_first[:, :, first : first + GROUP] for first in range(QUARTER, HALF, GROUP)}
         for entry in range(HALF, S, QUARTER):
             raw = keep.tile([P, PACK, QUARTER], F32, name="pos%d" % entry, align_bytes=64)
             nc.sync.dma_start(out=raw[:], in_=pos_rows[:, :, entry : entry + QUARTER])
@@ -102,13 +100,10 @@ def tile_picked_embpos_none_e_kernel(tc, xT, w1, w2_words, w2_scales, pos, offs,
             for at in range(0, n, GROUP):
                 x_codes[g][first + at] = (codes[:, at:], scale_bytes[:, at:])
 
-        starts_x = [sum(PIECES[:c]) for c in range(len(PIECES))]
         laid = [
             [keep.tile([P, n * PACK], BF16, name="laid", tag="laid%d_%d" % (g, c), align_bytes=64) for c, n in enumerate(widths)]
-            for g, widths in enumerate(((HALF, HALF), (QUARTER, QUARTER, QUARTER + GROUP)))
+            for g, widths in enumerate(((HALF, HALF), (QUARTER, QUARTER, QUARTER)))
         ]
-        late = laid[1][2]
-        laid[1][2:] = [late[:, : QUARTER * PACK], late[:, QUARTER * PACK :]]
         for u in range(2):
             pair = keep.tile([P, 2, S], BF16, name="pair%d" % u, align_bytes=64)
             for e in range(2):
@@ -120,19 +115,19 @@ def tile_picked_embpos_none_e_kernel(tc, xT, w1, w2_words, w2_scales, pos, offs,
         for c, tile in enumerate(laid[0]):
             quantise_x(0, c * HALF, HALF, tile, "x_codes0_%d" % c)
 
-        picked = [keep.tile([P, PACK, n], BF16, name="picked%d" % c, align_bytes=64) for c, n in enumerate(PIECES)]
+        picked = [keep.tile([P, PACK, QUARTER], BF16, name="picked%d" % c, align_bytes=64) for c in range(4)]
         for j in range(PACK):
-            for c, n in enumerate(PIECES):
-                gather(c not in ON_VECTOR[j], planes[PACK + j], picked[c][:, j, :], starts_x[c], n)
+            for c in range(4):
+                gather(c not in ON_VECTOR[j], planes[PACK + j], picked[c][:, j, :], c * QUARTER, QUARTER)
             if j == 1:
-                for c in range(len(PIECES) - 1):
+                for c in range(3):
                     weave(nc.vector.tensor_copy, laid[1][c], 0, picked[c][:, :2])
 
         weave(nc.vector.tensor_copy, laid[1][0], 1, picked[0][:, 2:])
         weave(nc.vector.tensor_copy, laid[1][1], 1, picked[1][:, 2:])
-        weave(nc.vector.tensor_copy, laid[1][2], 1, picked[2][:, 2:])
+        weave(nc.vector.tensor_copy, laid[1][2][:, : GROUP * PACK], 1, picked[2][:, 2:, :GROUP])
         quantise_x(1, 0, QUARTER, laid[1][0], "x_codes1_0")
-        weave(nc.scalar.copy, laid[1][3], 1, picked[3][:, 2:])
+        weave(nc.scalar.copy, laid[1][2][:, GROUP * PACK :], 1, picked[2][:, 2:, GROUP:])
 
         w1_tiles = {}
         w1_bf = {}
@@ -160,19 +155,29 @@ def tile_picked_embpos_none_e_kernel(tc, xT, w1, w2_words, w2_scales, pos, offs,
             for b in range(2):
                 w1_tiles[g, 2 * pair + b] = (codes[:, b * P : (b + 1) * P], scale_bytes[:, b * P : (b + 1) * P])
 
+        def lay_whole(g):
+            whole = keep.tile([P, GROUP * PACK], BF16, name="laid_last", tag="w1_raw%d" % g, align_bytes=64)
+            nc.scalar.copy(
+                out=whole[:].rearrange("p (c j) -> p c j", j=PACK),
+                in_=picked[3][:, :, g * GROUP : (g + 1) * GROUP].rearrange("p j c -> p c j"),
+            )
+            return whole
+
         round_w1(0, 0, 0)
         round_w1(0, 1, 5 * P // 8)
-        laid_last = keep.tile([P, GROUP * PACK], BF16, name="laid_last", tag="w1_raw0", align_bytes=64)
-        nc.scalar.copy(out=laid_last[:].rearrange("p (c j) -> p c j", j=PACK), in_=picked[4][:].rearrange("p j c -> p c j"))
+        laid_last = [lay_whole(0)]
         quantise_w1(0, 0)
         quantise_w1(0, 1)
         quantise_x(1, QUARTER, QUARTER, laid[1][1], "w1_bf0_0")
+        quantise_x(1, HALF, GROUP, laid[1][2][:, : GROUP * PACK], "w1_bf0_1")
         round_w1(1, 0, 0)
         round_w1(1, 1, 5 * P // 8)
+        laid_last.append(lay_whole(1))
         quantise_w1(1, 0)
         quantise_w1(1, 1)
-        quantise_x(1, starts_x[2], QUARTER + GROUP, late, "w1_bf1_0")
-        quantise_x(1, starts_x[4], PIECES[4], laid_last, "w1_bf1_1")
+        quantise_x(1, HALF + GROUP, GROUP, laid[1][2][:, GROUP * PACK :], "w1_bf1_0")
+        quantise_x(1, 3 * QUARTER, GROUP, laid_last[0], "w1_bf1_1")
+        quantise_x(1, S - GROUP, GROUP, laid_last[1], "x_codes1_last")
 
         warm = psum.tile([P, PACK, GROUP], F32, name="warm", tag="bank")
         for n in range(WARM_UPS):
@@ -201,56 +206,56 @@ def tile_picked_embpos_none_e_kernel(tc, xT, w1, w2_words, w2_scales, pos, offs,
                 )
             return acc
 
-        pair_sums = {}
-        for u in range(2):
-            for first in (0, QUARTER) if u == 0 else (QUARTER, 0):
-                steps = [(g, 2 * u + e) for g in range(PASSES) for e in range(2)]
-                pair_sums[first, u] = first_layer(first, QUARTER, steps[::-1] if (first, u) == (0, 1) else steps)
-        sums = {}
-        for first in range(HALF, S, GROUP):
-            sums[first] = first_layer(first, GROUP, [(g, t) for g in range(PASSES) for t in range(PACK)][::-1])
+        forward = [(g, t) for g in range(PASSES) for t in range(PACK)]
+        pair_sums = [first_layer(0, QUARTER, [step for step in forward if step[1] < 2])]
+        sums = {ON_GPSIMD: first_layer(ON_GPSIMD, GROUP, forward)}
+        pair_sums.append(first_layer(0, QUARTER, [step for step in forward if step[1] >= 2]))
+        for first in range(QUARTER, S, GROUP):
+            if first not in sums:
+                sums[first] = first_layer(first, GROUP, forward[::-1])
 
-        def add_pair(first, u, rounded):
-            pos_part = pos_pairs[u][:, :, first : first + QUARTER]
-            if (first, u) == (QUARTER, 0):
-                sum_laid = keep.tile([P, 2 * QUARTER], F32, name="sum_laid")
-                nc.scalar.copy(out=sum_laid[:].rearrange("p (c e) -> p c e", e=2), in_=pair_sums[first, u][:].rearrange("p e c -> p c e"))
+        def add_pair(u, rounded):
+            nc.vector.tensor_tensor(
+                out=rounded.rearrange("p (c i e) -> p c e i", i=RUN, e=2),
+                in0=pair_sums[u][:].rearrange("p e (c i) -> p c e i", i=RUN),
+                in1=pos_first[:, 2 * u : 2 * u + 2, :QUARTER].rearrange("p e (c i) -> p c e i", i=RUN),
+                op=ADD,
+            )
+
+        def add_pos(first, rounded):
+            if first == ON_GPSIMD:
+                sum_laid = keep.tile([P, GROUP * PACK], F32, name="sum_laid")
+                nc.scalar.copy(out=sum_laid[:].rearrange("p (c t) -> p c t", t=PACK), in_=sums[first][:].rearrange("p t c -> p c t"))
                 nc.gpsimd.tensor_tensor(
-                    out=rounded,
-                    in0=sum_laid[:].rearrange("p (c e) -> p c e", e=2),
-                    in1=pos_part.rearrange("p e c -> p c e"),
+                    out=rounded.rearrange("p (c t) -> p c t", t=PACK),
+                    in0=sum_laid[:].rearrange("p (c t) -> p c t", t=PACK),
+                    in1=pos_of[first].rearrange("p t c -> p c t"),
                     op=ADD,
                 )
             else:
                 nc.vector.tensor_tensor(
-                    out=rounded.rearrange("p (c i e) -> p c e i", i=RUN, e=2),
-                    in0=pair_sums[first, u][:].rearrange("p e (c i) -> p c e i", i=RUN),
-                    in1=pos_part.rearrange("p e (c i) -> p c e i", i=RUN),
+                    out=rounded.rearrange("p (c i t) -> p c t i", i=RUN, t=PACK),
+                    in0=sums[first][:].rearrange("p t (c i) -> p c t i", i=RUN),
+                    in1=pos_of[first].rearrange("p t (c i) -> p c t i", i=RUN),
                     op=ADD,
                 )
-
-        def add_pos(first, rounded):
-            nc.vector.tensor_tensor(
-                out=rounded.rearrange("p (c i t) -> p c t i", i=RUN, t=PACK),
-                in0=sums[first][:].rearrange("p t (c i) -> p c t i", i=RUN),
-                in1=pos_of[first].rearrange("p t (c i) -> p c t i", i=RUN),
-                op=ADD,
-            )
 
         def second_layer(first, n, rounded, tag, staged):
             h_codes = keep.tile([P, n], U32, name="h_codes", tag=tag, align_bytes=64)
             h_bytes = keep.tile([P, n], U8, name="h_bytes%d" % first, align_bytes=64)
             nc.vector.quantize_mx(out=h_codes[:].bitcast(FP8X4), scales=h_bytes[:], in_=rounded)
             res = psum.tile([P, n], F32, name="res", tag="bank")
-            nc.tensor.matmul_mx(
-                out=res[:],
-                lhsT=w2_codes[:].bitcast(FP8X4),
-                lhsT_scale=w2_bytes[:],
-                rhs=h_codes[:].bitcast(FP8X4),
-                rhs_scale=h_bytes[:],
-                start=True,
-                stop=True,
-            )
+            for at in range(0, n, QUARTER):
+                end = min(at + QUARTER, n)
+                nc.tensor.matmul_mx(
+                    out=res[:, at:end],
+                    lhsT=w2_codes[:].bitcast(FP8X4),
+                    lhsT_scale=w2_bytes[:],
+                    rhs=h_codes[:, at:end].bitcast(FP8X4),
+                    rhs_scale=h_bytes[:, at:end],
+                    start=True,
+                    stop=True,
+                )
             nc.scalar.copy(out=staged, in_=res[:])
 
         h_bf = [keep.tile([P, n * PACK], BF16, name="h_bf%d" % k, align_bytes=64) for k, n in enumerate(H_TILES)]
@@ -263,18 +268,16 @@ def tile_picked_embpos_none_e_kernel(tc, xT, w1, w2_words, w2_scales, pos, offs,
 
         h_words = h_bf[0][:].bitcast(U32).rearrange("p (c u) -> p c u", u=2)
         both = keep.tile([P, 2, 2 * QUARTER], BF16, name="h_pairs", align_bytes=64)
-        upper = keep.tile([P, 2 * QUARTER], BF16, name="h_upper", align_bytes=64)
-        add_pair(0, 0, both[:, 0, :])
-        add_pair(QUARTER, 0, h_bf[0][:].rearrange("p (c u e) -> p u c e", u=2, e=2)[:, 0, QUARTER:])
-        add_pair(QUARTER, 1, upper[:])
-        add_pair(0, 1, both[:, 1, :])
-        nc.scalar.copy(out=h_words[:, QUARTER:, 1], in_=upper[:].bitcast(U32))
+        add_pair(0, both[:, 0, :])
+        add_group(ON_GPSIMD)
+        add_pair(1, both[:, 1, :])
         nc.scalar.copy(
             out=h_words[:, :QUARTER],
             in_=both[:].rearrange("p u w -> p (u w)").bitcast(U32).rearrange("p (u c) -> p c u", u=2),
         )
-        for first in range(HALF, 6 * GROUP, GROUP):
-            add_group(first)
+        for first in range(QUARTER, 6 * GROUP, GROUP):
+            if first != ON_GPSIMD:
+                add_group(first)
         for k in range(2):
             staged = keep.tile([P, H_TILES[k]], F32, name="staged%d" % k)
             second_layer(starts[k], H_TILES[k], h_bf[k][:], "h_codes%d" % k, staged[:])

@@ -70,7 +70,7 @@ def tile_picked_embpos_none_e_kernel(tc, xT, w1, w2_words, w2_scales, pos, offs,
             nc.sync.dma_start(out=raw[:], in_=pos_rows[:, :, entry : entry + QUARTER])
             for at in range(0, QUARTER, GROUP):
                 pos_of[entry + at] = raw[:, :, at : at + GROUP]
-            if entry == HALF:
+            if entry == S - QUARTER:
                 nc.sync.dma_start(out=w2_codes[:].bitcast(I32), in_=w2_words[0].rearrange("p n t -> p (n t)").bitcast(I32))
                 for q in range(P // QUADRANT):
                     nc.sync.dma_start(
@@ -212,7 +212,8 @@ def tile_picked_embpos_none_e_kernel(tc, xT, w1, w2_words, w2_scales, pos, offs,
         pair_sums.append(first_layer(0, QUARTER, [step for step in forward if step[1] >= 2]))
         for first in range(QUARTER, S, GROUP):
             if first not in sums:
-                sums[first] = first_layer(first, GROUP, forward[::-1])
+                steps = forward[:PACK] + forward[PACK:][::-1] if first == QUARTER else forward[::-1]
+                sums[first] = first_layer(first, GROUP, steps)
 
         def add_pair(u, rounded):
             nc.vector.tensor_tensor(

@@ -29,6 +29,7 @@ QUARTER = S // 4
 ON_SCALAR = (512, 512, 768, 512)
 ON_VECTOR = ((), (2, 3), (0,), (0,))
 WARM_UPS = 7
+POS_LOADS = (GROUP, GROUP, QUARTER)
 H_TILES = (3 * GROUP, 3 * GROUP, GROUP, GROUP)
 ON_GPSIMD = 3 * GROUP
 
@@ -43,6 +44,11 @@ def tile_picked_embpos_none_e_kernel(tc, xT, w1, w2_words, w2_scales, pos, offs,
         w2_codes = keep.tile([P, N], U32, name="w2_codes", align_bytes=64)
         w2_bytes = keep.tile([P, N], U8, name="w2_bytes", align_bytes=64)
         nc.gpsimd.memset(w2_bytes[:], 0)
+        for q in range(P // QUADRANT):
+            nc.scalar.dma_start(
+                out=w2_bytes[QUADRANT * q : QUADRANT * q + 4, :].bitcast(I32),
+                in_=w2_scales[0][4 * q : 4 * q + 4, :].bitcast(I32),
+            )
 
         planes = []
         for g in range(PASSES):
@@ -65,18 +71,14 @@ def tile_picked_embpos_none_e_kernel(tc, xT, w1, w2_words, w2_scales, pos, offs,
         for u in range(2):
             nc.sync.dma_start(out=pos_first[:, 2 * u : 2 * u + 2, :], in_=pos_rows[:, 2 * u : 2 * u + 2, :HALF])
         pos_of = {first: pos_first[:, :, first : first + GROUP] for first in range(QUARTER, HALF, GROUP)}
-        for entry in range(HALF, S, QUARTER):
-            raw = keep.tile([P, PACK, QUARTER], F32, name="pos%d" % entry, align_bytes=64)
-            nc.sync.dma_start(out=raw[:], in_=pos_rows[:, :, entry : entry + QUARTER])
-            for at in range(0, QUARTER, GROUP):
+        entry = HALF
+        for n in POS_LOADS:
+            raw = keep.tile([P, PACK, n], F32, name="pos%d" % entry, align_bytes=64)
+            nc.sync.dma_start(out=raw[:], in_=pos_rows[:, :, entry : entry + n])
+            for at in range(0, n, GROUP):
                 pos_of[entry + at] = raw[:, :, at : at + GROUP]
-            if entry == S - QUARTER:
-                nc.sync.dma_start(out=w2_codes[:].bitcast(I32), in_=w2_words[0].rearrange("p n t -> p (n t)").bitcast(I32))
-                for q in range(P // QUADRANT):
-                    nc.sync.dma_start(
-                        out=w2_bytes[QUADRANT * q : QUADRANT * q + 4, :].bitcast(I32),
-                        in_=w2_scales[0][4 * q : 4 * q + 4, :].bitcast(I32),
-                    )
+            entry = entry + n
+        nc.sync.dma_start(out=w2_codes[:].bitcast(I32), in_=w2_words[0].rearrange("p n t -> p (n t)").bitcast(I32))
 
         def gather(on_scalar, plane, dst, first, n):
             picked = plane[:].indirect(offsets[:, first // PER_COLUMN : (first + n) // PER_COLUMN])

from contextlib import ExitStack

import concourse.mybir as mybir

K, T, S, H, N = 1024, 2048, 1024, 512, 128
FLOPS = 2 * K * H * S + 2 * H * N * S

F32 = mybir.dt.float32
BF16 = mybir.dt.bfloat16
I32 = mybir.dt.int32
U32 = mybir.dt.uint32
U16 = mybir.dt.uint16
U8 = mybir.dt.uint8
FP8X4 = mybir.dt.float8_e4m3fn_x4
COPY = mybir.ActivationFunctionType.Copy
ADD = mybir.AluOpType.add

P = 128
PACK = 4
K_PASS = P * PACK
PASSES = K // K_PASS
QUADRANT = 32
PER_COLUMN = 16
RUN = 2
GROUP = 128
HALF = S // 2
QUARTER = S // 4

ON_SCALAR = (512, 512, 768, 512)
ON_VECTOR = ((), (2, 3), (0,), (0,))
WARM_UPS = 7
POS_LOADS = (GROUP, GROUP, QUARTER)
H_TILES = (3 * GROUP, 3 * GROUP, GROUP, GROUP)
ON_GPSIMD = 3 * GROUP


def tile_picked_embpos_none_e_kernel(tc, xT, w1, w2_words, w2_scales, pos, offs, out):
    nc = tc.nc
    with ExitStack() as ctx:
        keep = ctx.enter_context(tc.tile_pool(name="keep", bufs=1))
        psum = ctx.enter_context(tc.psum_pool(name="psum", bufs=8))

        offsets = keep.tile([P, S // PER_COLUMN], U16, name="offsets")
        w2_codes = keep.tile([P, N], U32, name="w2_codes", align_bytes=64)
        w2_bytes = keep.tile([P, N], U8, name="w2_bytes", align_bytes=64)
        nc.gpsimd.memset(w2_bytes[:], 0)
        for q in range(P // QUADRANT):
            nc.scalar.dma_start(
                out=w2_bytes[QUADRANT * q : QUADRANT * q + 4, :].bitcast(I32),
                in_=w2_scales[0][4 * q : 4 * q + 4, :].bitcast(I32),
            )

        planes = []
        for g in range(PASSES):
            rows = xT[g * K_PASS : (g + 1) * K_PASS, :].rearrange("(p j) s -> p j s", j=PACK)
            for j in range(PACK):
                plane = keep.tile([P, T], F32, name="plane%d_%d" % (g, j), align_bytes=64)
                nc.sync.dma_start(out=plane[:], in_=rows[:, j, :])
                if not planes:
                    nc.sync.dma_start(offsets[:], offs)
                planes.append(plane)

        w1_raw = []
        for g in range(PASSES):
            raw = keep.tile([P, PACK, H], F32, name="w1_raw", tag="w1_raw%d" % g, align_bytes=64)
            nc.sync.dma_start(out=raw[:], in_=w1[g * K_PASS : (g + 1) * K_PASS, :].rearrange("(p j) i -> p j i", j=PACK))
            w1_raw.append(raw)

        pos_rows = pos.rearrange("(p t) s -> p t s", t=PACK)
        pos_first = keep.tile([P, PACK, HALF], F32, name="pos_first", align_bytes=64)
        for u in range(2):
            nc.sync.dma_start(out=pos_first[:, 2 * u : 2 * u + 2, :], in_=pos_rows[:, 2 * u : 2 * u + 2, :HALF])
        pos_of = {first: pos_first[:, :, first : first + GROUP] for first in range(QUARTER, HALF, GROUP)}
        entry = HALF
        for n in POS_LOADS:
            raw = keep.tile([P, PACK, n], F32, name="pos%d" % entry, align_bytes=64)
            nc.sync.dma_start(out=raw[:], in_=pos_rows[:, :, entry : entry + n])
            for at in range(0, n, GROUP):
                pos_of[entry + at] = raw[:, :, at : at + GROUP]
            entry = entry + n
        nc.sync.dma_start(out=w2_codes[:].bitcast(I32), in_=w2_words[0].rearrange("p n t -> p (n t)").bitcast(I32))

        def gather(on_scalar, plane, dst, first, n):
            picked = plane[:].indirect(offsets[:, first // PER_COLUMN : (first + n) // PER_COLUMN])
            if on_scalar:
                nc.scalar.activation(out=dst, in_=picked, func=COPY)
            else:
                nc.vector.tensor_copy(out=dst, in_=picked)

        def weave(copy, laid, u, pair):
            copy(
                out=laid[:].rearrange("p (c u e) -> p u c e", u=2, e=2)[:, u],
                in_=pair.rearrange("p e c -> p c e"),
            )

        x_codes = [{} for g in range(PASSES)]

        def quantise_x(g, first, n, laid, tag):
            codes = keep.tile([P, n], U32, name="x_codes", tag=tag, align_bytes=64)
            scale_bytes = keep.tile([P, n], U8, name="x_bytes%d_%d" % (g, first), align_bytes=64)
            nc.vector.quantize_mx(out=codes[:].bitcast(FP8X4), scales=scale_bytes[:], in_=laid[:])
            for at in range(0, n, GROUP):
                x_codes[g][first + at] = (codes[:, at:], scale_bytes[:, at:])

        laid = [
            [keep.tile([P, n * PACK], BF16, name="laid", tag="laid%d_%d" % (g, c), align_bytes=64) for c, n in enumerate(widths)]
            for g, widths in enumerate(((HALF, HALF), (QUARTER, QUARTER, QUARTER)))
        ]
        for u in range(2):
            pair = keep.tile([P, 2, S], BF16, name="pair%d" % u, align_bytes=64)
            for e in range(2):
                cut = ON_SCALAR[2 * u + e]
                gather(True, planes[2 * u + e], pair[:, e, :cut], 0, cut)
                gather(False, planes[2 * u + e], pair[:, e, cut:], cut, S - cut)
            for c, tile in enumerate(laid[0]):
                weave(nc.vector.tensor_copy, tile, u, pair[:, :, c * HALF : (c + 1) * HALF])
        for c, tile in enumerate(laid[0]):
            quantise_x(0, c * HALF, HALF, tile, "x_codes0_%d" % c)

        picked = [keep.tile([P, PACK, QUARTER], BF16, name="picked%d" % c, align_bytes=64) for c in range(4)]
        for j in range(PACK):
            for c in range(4):
                gather(c not in ON_VECTOR[j], planes[PACK + j], picked[c][:, j, :], c * QUARTER, QUARTER)
            if j == 1:
                for c in range(3):
                    weave(nc.vector.tensor_copy, laid[1][c], 0, picked[c][:, :2])

        weave(nc.vector.tensor_copy, laid[1][0], 1, picked[0][:, 2:])
        weave(nc.vector.tensor_copy, laid[1][1], 1, picked[1][:, 2:])
        weave(nc.vector.tensor_copy, laid[1][2][:, : GROUP * PACK], 1, picked[2][:, 2:, :GROUP])
        quantise_x(1, 0, QUARTER, laid[1][0], "x_codes1_0")
        weave(nc.scalar.copy, laid[1][2][:, GROUP * PACK :], 1, picked[2][:, 2:, GROUP:])

        w1_tiles = {}
        w1_bf = {}

        def round_w1(g, pair, cut):
            rounded = keep.tile([P, 2 * P * PACK], BF16, name="w1_bf", tag="w1_bf%d_%d" % (g, pair), align_bytes=64)
            dst = rounded[:].rearrange("p (b m j) -> p m j b", b=2, j=PACK)
            src = w1_raw[g][:].rearrange("p j (m a b) -> p a m j b", a=2, b=2)
            if cut > 0:
                nc.scalar.copy(out=dst[:, :cut], in_=src[:, pair, :cut])
            if cut < P:
                nc.vector.tensor_copy(out=dst[:, cut:], in_=src[:, pair, cut:])
            w1_bf[g, pair] = rounded

        def quantise_w1(g, pair):
            codes = keep.tile([P, 2 * P], U32, name="w1_codes%d_%d" % (g, pair), align_bytes=64)
            scale_bytes = keep.tile([P, 2 * P], U8, name="w1_bytes%d_%d" % (g, pair), align_bytes=64)
            step = P if (g, pair) == (0, 0) else 2 * P
            for at in range(0, 2 * P, step):
                nc.vector.quantize_mx(
                    out=codes[:, at : at + step].bitcast(FP8X4),
                    scales=scale_bytes[:, at : at + step],
                    in_=w1_bf[g, pair][:, at * PACK : (at + step) * PACK],
                )
            for b in range(2):
                w1_tiles[g, 2 * pair + b] = (codes[:, b * P : (b + 1) * P], scale_bytes[:, b * P : (b + 1) * P])

        def lay_whole(g):
            whole = keep.tile([P, GROUP * PACK], BF16, name="laid_last", tag="w1_raw%d" % g, align_bytes=64)
            nc.scalar.copy(
                out=whole[:].rearrange("p (c j) -> p c j", j=PACK),
                in_=picked[3][:, :, g * GROUP : (g + 1) * GROUP].rearrange("p j c -> p c j"),
            )
            return whole

        round_w1(0, 0, 0)
        round_w1(0, 1, 5 * P // 8)
        laid_last = [lay_whole(0)]
        quantise_w1(0, 0)
        quantise_w1(0, 1)
        quantise_x(1, QUARTER, QUARTER, laid[1][1], "w1_bf0_0")
        quantise_x(1, HALF, GROUP, laid[1][2][:, : GROUP * PACK], "w1_bf0_1")
        round_w1(1, 0, 0)
        round_w1(1, 1, 5 * P // 8)
        laid_last.append(lay_whole(1))
        quantise_w1(1, 0)
        quantise_w1(1, 1)
        quantise_x(1, HALF + GROUP, GROUP, laid[1][2][:, GROUP * PACK :], "w1_bf1_0")
        quantise_x(1, 3 * QUARTER, GROUP, laid_last[0], "w1_bf1_1")
        quantise_x(1, S - GROUP, GROUP, laid_last[1], "x_codes1_last")

        warm = psum.tile([P, PACK, GROUP], F32, name="warm", tag="bank")
        for n in range(WARM_UPS):
            codes, scale_bytes = (part[:, :GROUP] for part in x_codes[1][0])
            nc.tensor.matmul_mx(
                out=warm[:, n % PACK, :],
                lhsT=codes.bitcast(FP8X4),
                lhsT_scale=scale_bytes,
                rhs=codes.bitcast(FP8X4),
                rhs_scale=scale_bytes,
                start=True,
                stop=True,
            )
        def first_layer(first, n, steps):
            low = min(t for g, t in steps)
            acc = psum.tile([P, len(steps) // PASSES, n], F32, name="acc", tag="bank")
            for g, t in steps:
                nc.tensor.matmul_mx(
                    out=acc[:, t - low, :],
                    lhsT=w1_tiles[g, t][0].bitcast(FP8X4),
                    lhsT_scale=w1_tiles[g, t][1],
                    rhs=x_codes[g][first][0][:, :n].bitcast(FP8X4),
                    rhs_scale=x_codes[g][first][1][:, :n],
                    start=((g, t) == steps[0]),
                    stop=((g, t) == steps[-1]),
                )
            return acc

        forward = [(g, t) for g in range(PASSES) for t in range(PACK)]
        pair_sums = [first_layer(0, QUARTER, [step for step in forward if step[1] < 2])]
        sums = {ON_GPSIMD: first_layer(ON_GPSIMD, GROUP, forward)}
        pair_sums.append(first_layer(0, QUARTER, [step for step in forward if step[1] >= 2]))
        for first in range(QUARTER, S, GROUP):
            if first not in sums:
                steps = forward[:PACK] + forward[PACK:][::-1] if first == QUARTER else forward[::-1]
                sums[first] = first_layer(first, GROUP, steps)

        def add_pair(u, rounded):
            nc.vector.tensor_tensor(
                out=rounded.rearrange("p (c i e) -> p c e i", i=RUN, e=2),
                in0=pair_sums[u][:].rearrange("p e (c i) -> p c e i", i=RUN),
                in1=pos_first[:, 2 * u : 2 * u + 2, :QUARTER].rearrange("p e (c i) -> p c e i", i=RUN),
                op=ADD,
            )

        def add_pos(first, rounded):
            if first == ON_GPSIMD:
                sum_laid = keep.tile([P, GROUP * PACK], F32, name="sum_laid")
                nc.scalar.copy(out=sum_laid[:].rearrange("p (c t) -> p c t", t=PACK), in_=sums[first][:].rearrange("p t c -> p c t"))
                nc.gpsimd.tensor_tensor(
                    out=rounded.rearrange("p (c t) -> p c t", t=PACK),
                    in0=sum_laid[:].rearrange("p (c t) -> p c t", t=PACK),
                    in1=pos_of[first].rearrange("p t c -> p c t"),
                    op=ADD,
                )
            else:
                nc.vector.tensor_tensor(
                    out=rounded.rearrange("p (c i t) -> p c t i", i=RUN, t=PACK),
                    in0=sums[first][:].rearrange("p t (c i) -> p c t i", i=RUN),
                    in1=pos_of[first].rearrange("p t (c i) -> p c t i", i=RUN),
                    op=ADD,
                )

        def second_layer(first, n, rounded, tag, staged):
            h_codes = keep.tile([P, n], U32, name="h_codes", tag=tag, align_bytes=64)
            h_bytes = keep.tile([P, n], U8, name="h_bytes%d" % first, align_bytes=64)
            nc.vector.quantize_mx(out=h_codes[:].bitcast(FP8X4), scales=h_bytes[:], in_=rounded)
            res = psum.tile([P, n], F32, name="res", tag="bank")
            for at in range(0, n, QUARTER):
                end = min(at + QUARTER, n)
                nc.tensor.matmul_mx(
                    out=res[:, at:end],
                    lhsT=w2_codes[:].bitcast(FP8X4),
                    lhsT_scale=w2_bytes[:],
                    rhs=h_codes[:, at:end].bitcast(FP8X4),
                    rhs_scale=h_bytes[:, at:end],
                    start=True,
                    stop=True,
                )
            nc.scalar.copy(out=staged, in_=res[:])

        h_bf = [keep.tile([P, n * PACK], BF16, name="h_bf%d" % k, align_bytes=64) for k, n in enumerate(H_TILES)]
        starts = [sum(H_TILES[:k]) for k in range(len(H_TILES))]

        def add_group(first):
            k = max(k for k in range(len(H_TILES)) if starts[k] <= first)
            at = first - starts[k]
            add_pos(first, h_bf[k][:, at * PACK : (at + GROUP) * PACK])

        h_words = h_bf[0][:].bitcast(U32).rearrange("p (c u) -> p c u", u=2)
        both = keep.tile([P, 2, 2 * QUARTER], BF16, name="h_pairs", align_bytes=64)
        add_pair(0, both[:, 0, :])
        add_group(ON_GPSIMD)
        add_pair(1, both[:, 1, :])
        nc.scalar.copy(
            out=h_words[:, :QUARTER],
            in_=both[:].rearrange("p u w -> p (u w)").bitcast(U32).rearrange("p (u c) -> p c u", u=2),
        )
        for first in range(QUARTER, 6 * GROUP, GROUP):
            if first != ON_GPSIMD:
                add_group(first)
        for k in range(2):
            staged = keep.tile([P, H_TILES[k]], F32, name="staged%d" % k)
            second_layer(starts[k], H_TILES[k], h_bf[k][:], "h_codes%d" % k, staged[:])
            nc.sync.dma_start(out=out[:, starts[k] : starts[k + 1]], in_=staged[:])
        add_group(6 * GROUP)
        add_group(7 * GROUP)
        staged = keep.tile([P, S - starts[2]], F32, name="staged2")
        for k in range(2, len(H_TILES)):
            at = starts[k] - starts[2]
            second_layer(starts[k], H_TILES[k], h_bf[k][:], "h_codes%d" % k, staged[:, at : at + H_TILES[k]])
        nc.sync.dma_start(out=out[:, starts[2] :], in_=staged[:])
